import numpy as np
import ml_dtypes


def mxq(x, axis, fmt="e4m3"):
    dtype, down = {"e4m3": (ml_dtypes.float8_e4m3fn, 7), "e5m2": (ml_dtypes.float8_e5m2, 14)}[fmt]
    v = np.moveaxis(np.asarray(x, np.float32).astype(ml_dtypes.bfloat16).astype(np.float64), axis, -1)
    blocks = v.reshape(v.shape[:-1] + (-1, 32))
    amax = np.abs(blocks).max(-1, keepdims=True)
    byte = np.maximum(np.where(amax > 0, np.frexp(amax)[1] - 1 + 127, 0) - down, 1)
    scale = np.exp2(byte - 127.0)
    codes = (blocks / scale).astype(np.float32).astype(dtype).astype(np.float64)
    return np.moveaxis((codes * scale).reshape(v.shape), -1, axis)


WIDE = False


def mx_kscale(k):
    if not WIDE:
        return np.ones(k)
    levels = np.array([24, -24, 12, -12, 0])
    if k % 512:
        return np.exp2(np.random.permutation(np.resize(levels, k // 32))).repeat(32)
    a = np.empty((k // 512, 16))
    for p in range(k // 512):
        a[p, :8] = np.random.permutation(np.resize(levels, 8))
        for g in range(8):
            far = levels[np.abs(levels - a[p, g]) >= 10]
            a[p, g + 8] = far[np.random.randint(len(far))]
    return np.exp2(a.ravel()).repeat(32)


def f64(x):
    return np.asarray(x).astype(np.float64)


def striped(idx):
    return np.tile(idx.reshape(-1, 16).T, (8, 1)).astype(np.uint16)


def unstriped(offs):
    return offs[:16].T.reshape(-1).astype(np.int64)


E2M1 = np.array([0.0, 0.5, 1.0, 1.5, 2.0, 3.0, 4.0, 6.0, -0.0, -0.5, -1.0, -1.5, -2.0, -3.0, -4.0, -6.0])


def pack_weight(w, fmt):
    k, n = w.shape
    w = f64(np.asarray(w, np.float32).astype(ml_dtypes.bfloat16)).reshape(k // 32, 32, n)
    amax = np.abs(w).max(1)
    if fmt == "e4m3":
        byte = np.frexp(amax)[1] - 1 + 127 - 7
    else:
        mant, ex = np.frexp(amax / 6.0)
        byte = np.where(mant > 0.5, ex, ex - 1) + 127
    byte = np.clip(np.where(amax > 0, byte, 1), 1, 254)
    scaled = (w * np.exp2(127.0 - byte)[:, None, :]).reshape(k, n).astype(np.float32)
    by_word = np.ascontiguousarray(scaled.reshape(k // 512, 128, 4, n).transpose(0, 1, 3, 2))
    if fmt == "e4m3":
        words = by_word.astype(ml_dtypes.float8_e4m3fn).view(np.uint8)
    else:
        c = by_word.astype(ml_dtypes.float4_e2m1fn).view(np.uint8) & 0xF
        words = (c[..., 0::2] | (c[..., 1::2] << 4)).reshape(k // 512, 128, 2 * n)
    return np.ascontiguousarray(words), np.ascontiguousarray(byte.astype(np.uint8).reshape(k // 512, 16, n))


def unpack_weight(words, scales, fmt):
    g, _, n = scales.shape
    words = np.ascontiguousarray(words).reshape(g, 128, n, -1)
    if fmt == "e4m3":
        vals = words.view(ml_dtypes.float8_e4m3fn).astype(np.float64)
    else:
        nib = np.empty((g, 128, n, 4), np.uint8)
        nib[..., 0::2] = words & 0xF
        nib[..., 1::2] = words >> 4
        vals = E2M1[nib]
    vals = vals * np.repeat(np.exp2(scales.astype(np.float64) - 127.0), 8, axis=1)[..., None]
    return vals.transpose(0, 1, 3, 2).reshape(g * 512, n)


def pack_table4(v):
    words, scales = pack_weight(v, "e2m1")
    g, t = words.shape[0] // 2, v.shape[1]
    return np.ascontiguousarray(words.reshape(g, 2, 128, t, 2).transpose(0, 2, 3, 1, 4).reshape(g, 128, t, 4)), scales


def unpack_table4(words, scales):
    g, _, t, _ = words.shape
    return unpack_weight(words.reshape(g, 128, t, 2, 2).transpose(0, 3, 1, 2, 4).reshape(2 * g, 128, 2 * t), scales, "e2m1")


def planes(y):
    n, m = y.shape
    v = y.astype(np.float32).astype(ml_dtypes.bfloat16).astype(np.float64).reshape(n // 32, 32, m)
    top = np.abs(v).max(1)
    byte = np.clip(np.where(top > 0, np.frexp(top)[1] - 1 + 127 - 7, 1), 1, 254)
    codes = (v * np.exp2(127.0 - byte)[:, None, :]).reshape(n, m).astype(np.float32).astype(ml_dtypes.float8_e4m3fn).view(np.uint8)
    words = codes.reshape(n // 512, 128, 4, m).transpose(0, 1, 3, 2)
    return np.ascontiguousarray(words), np.ascontiguousarray(byte.astype(np.uint8).reshape(n // 512, 16, m))


def silu(f):
    return f / (1.0 + np.exp(-np.maximum(f, -700.0)))


def sigm(f):
    return 1.0 / (1.0 + np.exp(-np.maximum(f, -700.0)))


K, N, T, J = 1024, 512, 4096, 1024


def setup_inputs():
    n = np.random.standard_normal
    s = mx_kscale(K)[:, None]
    p_tab = pack_table4(n((K, T)) * s)
    p_wg = pack_weight(n((K, N)) / np.sqrt(K) / s, "e4m3")
    p_wh4 = pack_weight(n((K, N)) / np.sqrt(K) / s, "e2m1")
    return {
        "tab_words": p_tab[0],
        "tab_scales": p_tab[1],
        "wg_words": p_wg[0],
        "wg_scales": p_wg[1],
        "wh4_words": p_wh4[0],
        "wh4_scales": p_wh4[1],
        "whd": (0.4 * (n((K, N)) / np.sqrt(K) / s)).astype(np.float32),
        "bg": (0.3 * n(N) - 1.0).astype(np.float32),
        "rT": (n((N, T))).astype(np.float32),
        "offs": striped(np.random.permutation(T)[:J]),
    }


def reference(tab_words, tab_scales, wg_words, wg_scales, wh4_words, wh4_scales, whd, bg, rT, offs):
    idx = unstriped(offs)
    tab_ = unpack_table4(tab_words, tab_scales)[:, idx]
    wg_ = unpack_weight(wg_words, wg_scales, "e4m3")
    wh4_ = unpack_weight(wh4_words, wh4_scales, "e2m1")
    whd_ = mxq(f64(whd), 0, "e4m3")
    ga = wg_.T @ tab_
    gate = sigm(ga + f64(bg)[:, None])
    ha = wh4_.T @ tab_ + whd_.T @ tab_
    out_0 = f64(rT)[:, idx] + gate * (silu(ha) - f64(rT)[:, idx])
    return (out_0,) + planes(out_0)

@@ -1,0 +1,226 @@
+from contextlib import ExitStack
+
+import concourse.mybir as mybir
+
+K, N, T, J = 1024, 512, 4096, 1024
+FLOPS = 3 * 2 * K * N * J
+
+F32 = mybir.dt.float32
+BF16 = mybir.dt.bfloat16
+I32 = mybir.dt.int32
+U32 = mybir.dt.uint32
+U16 = mybir.dt.uint16
+U8 = mybir.dt.uint8
+FP8X4 = mybir.dt.float8_e4m3fn_x4
+FP4X4 = mybir.dt.float4_e2m1fn_x4
+ALU = mybir.AluOpType
+ACT = mybir.ActivationFunctionType
+
+P = 128
+PACK = 4
+PASSES = K // (P * PACK)
+BANK = 512
+HALVES = J // BANK
+LAST_CHUNKS = (256, 256, 256, 128, 128)
+
+
+def tile_list_hwayt_dl_siluP_kernel(
+    tc, tab_words, tab_scales, wg_words, wg_scales, wh4_words, wh4_scales, whd, bg, rT, offs, out_0, out_1, out_2
+):
+    nc = tc.nc
+    with ExitStack() as ctx:
+        keep = ctx.enter_context(tc.tile_pool(name="keep", bufs=1))
+        psum = ctx.enter_context(tc.psum_pool(name="psum", bufs=1))
+
+        offsets = keep.tile([P, J // 16], U16, name="offsets")
+        nc.sync.dma_start(offsets[:], offs)
+
+        bias = keep.tile([P, PACK], F32, name="bias")
+        nc.sync.dma_start(bias[:], bg.rearrange("(p t) -> p t", t=PACK))
+        warm = keep.tile([P, 1], F32, name="warm", tag="tab", align_bytes=64)
+        warm_out = keep.tile([P, 1], F32, name="warm_out", tag="whd0", align_bytes=64)
+
+        tab_planes = keep.tile([P, PASSES * T // 4], I32, name="tab_planes", tag="r2", align_bytes=64)
+        nc.vector.memset(tab_planes[:], 0)
+        nc.vector.memset(warm[:], 0.0)
+        nc.scalar.activation(warm_out[:], warm[:], ACT.Sigmoid)
+        for q in range(4):
+            nc.sync.dma_start(
+                tab_planes[32 * q : 32 * q + 4, :].rearrange("r (a c) -> r a c", a=PASSES),
+                tab_scales[:, 4 * q : 4 * q + 4, :].bitcast(I32).rearrange("a r c -> r a c"),
+            )
+
+        def load_planes(scales, tag):
+            planes = keep.tile([P, PASSES * N // 4], I32, name="w_planes", tag=tag, align_bytes=64)
+            nc.vector.memset(planes[:], 0)
+            for q in range(4):
+                nc.scalar.dma_start(
+                    planes[32 * q : 32 * q + 4, :].rearrange("r (a c) -> r a c", a=PASSES),
+                    scales[:, 4 * q : 4 * q + 4, :].bitcast(I32).rearrange("a r c -> r a c"),
+                )
+            return planes
+
+        w_planes = (load_planes(wg_scales, "r1"), load_planes(wh4_scales, "wh4_planes"))
+
+        wg_raw = keep.tile([P, PASSES, N], I32, name="wg_raw", tag="whd1", align_bytes=64)
+        nc.sync.dma_start(wg_raw[:], wg_words.rearrange("a p n i -> p a (n i)").bitcast(I32))
+        wh4_raw = keep.tile([P, PASSES, N // 2], I32, name="wh4_raw", tag="r0", align_bytes=64)
+        nc.sync.dma_start(wh4_raw[:], wh4_words.rearrange("a p c -> p a c").bitcast(I32))
+        tab = keep.tile([P, T], I32, name="tab", tag="tab", align_bytes=64)
+        nc.sync.dma_start(tab[:], tab_words[0].rearrange("p c i -> p (c i)").bitcast(I32))
+        v_scales = []
+        for a in range(PASSES):
+            got = keep.tile([P, J], U8, name="v_scales%d" % a, align_bytes=64)
+            nc.vector.tensor_copy(got[:], tab_planes[:].bitcast(U8)[:, a * T : (a + 1) * T].indirect(offsets[:]))
+            v_scales.append(got)
+
+        wg_dealt = keep.tile([P, PASSES, N], I32, name="wg_dealt", align_bytes=64)
+        nc.vector.tensor_copy(
+            wg_dealt[:].rearrange("p a (t m) -> p a m t", t=PACK),
+            wg_raw[:].rearrange("p a (m t) -> p a m t", t=PACK),
+        )
+        wh4_dealt = keep.tile([P, PASSES, N], U16, name="wh4_dealt", align_bytes=64)
+        nc.vector.tensor_copy(
+            wh4_dealt[:].rearrange("p a (t m) -> p a m t", t=PACK),
+            wh4_raw[:].bitcast(U16).rearrange("p a (m t) -> p a m t", t=PACK),
+        )
+        w_scales = []
+        for w, planes in enumerate(w_planes):
+            dealt = keep.tile([P, PASSES, N], U8, name="w_scales%d" % w, align_bytes=64)
+            nc.vector.tensor_copy(
+                dealt[:].rearrange("p a (t m) -> p a m t", t=PACK),
+                planes[:].bitcast(U8).rearrange("p (a m t) -> p a m t", a=PASSES, t=PACK),
+            )
+            w_scales.append(dealt)
+        neg_bias = keep.tile([P, PACK], F32, name="neg_bias")
+        nc.vector.tensor_scalar(neg_bias[:], bias[:], -1.0, None, ALU.mult)
+
+        v_words = []
+        for h in range(HALVES):
+            pairs = keep.tile([P, BANK], I32, name="pairs%d" % h, tag=("r3", "pairs1")[h], align_bytes=64)
+            nc.vector.tensor_copy(
+                pairs[:].bitcast(U32), tab[:].bitcast(U32).indirect(offsets[:, h * 32 : (h + 1) * 32])
+            )
+            parted = keep.tile([P, PASSES, BANK], U16, name="parted%d" % h, align_bytes=64)
+            nc.vector.tensor_copy(parted[:], pairs[:].bitcast(U16).rearrange("p (j d) -> p d j", d=PASSES))
+            v_words.append(parted)
+
+        whd_raw = []
+        for a in range(PASSES):
+            raw = keep.tile([P, PACK, N], F32, name="whd_raw%d" % a, tag="whd%d" % a, align_bytes=64)
+            nc.sync.dma_start(raw[:], whd[a * 512 : (a + 1) * 512, :].rearrange("(p i) n -> p i n", i=PACK))
+            whd_raw.append(raw)
+        r_rows = rT.rearrange("(p t) c -> p t c", t=PACK)
+        r_tiles = []
+        for t in range(PACK):
+            r_tile = keep.tile([P, T], F32, name="r_tile%d" % t, tag="r%d" % t, align_bytes=64)
+            nc.sync.dma_start(r_tile[:], r_rows[:, t, :])
+            r_tiles.append(r_tile)
+
+        def moving(a, h):
+            return dict(
+                rhs=v_words[h][:, a, :].bitcast(U8).bitcast(FP4X4),
+                rhs_scale=v_scales[a][:, h * BANK : (h + 1) * BANK],
+            )
+
+        whd_codes = keep.tile([P, PASSES, N], U32, name="whd_codes", align_bytes=64)
+        whd_scales = keep.tile([P, PASSES, N], U8, name="whd_scales", align_bytes=64)
+        for a in range(PASSES):
+            grouped = keep.tile([P, N * PACK], BF16, name="whd_grouped%d" % a, align_bytes=64)
+            nc.scalar.copy(
+                grouped[:].rearrange("p (t m i) -> p m i t", t=PACK, i=PACK),
+                whd_raw[a][:].rearrange("p i (m t) -> p m i t", t=PACK),
+            )
+            nc.vector.quantize_mx(out=whd_codes[:, a, :].bitcast(FP8X4), scales=whd_scales[:, a, :], in_=grouped[:])
+
+        carry = keep.tile([P, PACK, J], F32, name="carry")
+        for h in range(HALVES):
+            for t in range(PACK):
+                ga = psum.tile([P, BANK], F32, name="bank%d" % (2 * t + h))
+                cols = slice(t * P, (t + 1) * P)
+                for a in range(PASSES):
+                    nc.tensor.matmul_mx(
+                        out=ga[:],
+                        lhsT=wg_dealt[:, a, cols].bitcast(FP8X4),
+                        lhsT_scale=w_scales[0][:, a, cols],
+                        start=(a == 0),
+                        stop=(a == PASSES - 1),
+                        **moving(a, h),
+                    )
+                nc.scalar.activation(
+                    carry[:, t, h * BANK : (h + 1) * BANK], ga[:], ACT.Sigmoid, bias=neg_bias[:, t : t + 1], scale=-1.0
+                )
+
+        made = keep.tile([P, PACK, J], F32, name="made")
+        for t in range(PACK):
+            cols = slice(t * P, (t + 1) * P)
+            for h in range(HALVES):
+                ha = psum.tile([P, BANK], F32, name="bank%d" % (2 * t + h))
+                for a in range(PASSES):
+                    nc.tensor.matmul_mx(
+                        out=ha[:],
+                        lhsT=wh4_dealt[:, a, cols].bitcast(U8).bitcast(FP4X4),
+                        lhsT_scale=w_scales[1][:, a, cols],
+                        start=(a == 0),
+                        stop=False,
+                        **moving(a, h),
+                    )
+                for a in range(PASSES):
+                    nc.tensor.matmul_mx(
+                        out=ha[:],
+                        lhsT=whd_codes[:, a, cols].bitcast(FP8X4),
+                        lhsT_scale=whd_scales[:, a, cols],
+                        start=False,
+                        stop=(a == PASSES - 1),
+                        **moving(a, h),
+                    )
+                nc.scalar.activation(made[:, t, h * BANK : (h + 1) * BANK], ha[:], ACT.Silu)
+
+        y = keep.tile([P, PACK, J], F32, name="y")
+        y_rows = out_0.rearrange("(p t) j -> p t j", t=PACK)
+        for t in range(PACK):
+            nc.vector.scalar_tensor_tensor(
+                made[:, t, :], carry[:, t, :], 1.0, made[:, t, :], ALU.subtract, ALU.mult
+            )
+            if t < PACK - 1:
+                nc.vector.tensor_tensor(y[:, t, :], r_tiles[t][:].indirect(offsets[:]), carry[:, t, :], ALU.mult)
+                nc.vector.tensor_tensor(y[:, t, :], y[:, t, :], made[:, t, :], ALU.subtract)
+                nc.sync.dma_start(y_rows[:, t, :], y[:, t, :])
+
+        y_round = keep.tile([P, J * PACK], BF16, name="y_round", align_bytes=64)
+        y_codes = keep.tile([P, J], I32, name="y_codes", align_bytes=64)
+        y_scales = keep.tile([P, J], U8, name="y_scales", align_bytes=64)
+        code_rows = out_1[0].rearrange("p j i -> p (j i)").bitcast(I32)
+        t = PACK - 1
+        j0 = 0
+        pending = None
+
+        def finish(js):
+            nc.vector.quantize_mx(
+                out=y_codes[:, js].bitcast(FP8X4),
+                scales=y_scales[:, js],
+                in_=y_round[:, js.start * PACK : js.stop * PACK],
+            )
+            nc.sync.dma_start(code_rows[:, js], y_codes[:, js])
+
+        for width in LAST_CHUNKS:
+            js = slice(j0, j0 + width)
+            nc.vector.tensor_tensor(
+                y[:, t, js], r_tiles[t][:].indirect(offsets[:, j0 // 16 : (j0 + width) // 16]), carry[:, t, js], ALU.mult
+            )
+            nc.vector.tensor_tensor(y[:, t, js], y[:, t, js], made[:, t, js], ALU.subtract)
+            nc.sync.dma_start(y_rows[:, t, js], y[:, t, js])
+            nc.scalar.copy(
+                y_round[:, j0 * PACK : (j0 + width) * PACK].rearrange("p (c i t) -> p c t i", i=4, t=PACK),
+                y[:, :, js].rearrange("p t (c i) -> p c t i", i=4),
+            )
+            if pending is not None:
+                finish(pending)
+            pending = js
+            j0 = j0 + width
+        finish(pending)
+        for q in range(4):
+            queue = nc.scalar if q % 2 else nc.sync
+            queue.dma_start(
+                out_2[0, 4 * q : 4 * q + 4, :].bitcast(I32), y_scales[32 * q : 32 * q + 4, :].bitcast(I32)
+            )

@@ -22,6 +22,7 @@ PASSES = K // (P * PACK)
 BANK = 512
 HALVES = J // BANK
 LAST_CHUNKS = (256, 256, 256, 128, 128)
+STORE_FROM = {512: 0, 768: 512, 1024: 768}
 
 
 def tile_list_hwayt_dl_siluP_kernel(
@@ -35,12 +36,12 @@ def tile_list_hwayt_dl_siluP_kernel(
         offsets = keep.tile([P, J // 16], U16, name="offsets")
         nc.sync.dma_start(offsets[:], offs)
 
-        bias = keep.tile([P, PACK], F32, name="bias")
-        nc.sync.dma_start(bias[:], bg.rearrange("(p t) -> p t", t=PACK))
+        bias = keep.tile([P, PACK], F32, name="bias", tag="wh4_planes", align_bytes=64)
+        nc.scalar.dma_start(bias[:], bg.rearrange("(p t) -> p t", t=PACK))
         warm = keep.tile([P, 1], F32, name="warm", tag="tab", align_bytes=64)
-        warm_out = keep.tile([P, 1], F32, name="warm_out", tag="whd0", align_bytes=64)
+        warm_out = keep.tile([P, 1], F32, name="warm_out", tag="r2", align_bytes=64)
 
-        tab_planes = keep.tile([P, PASSES * T // 4], I32, name="tab_planes", tag="r2", align_bytes=64)
+        tab_planes = keep.tile([P, PASSES * T // 4], I32, name="tab_planes", tag="r0", align_bytes=64)
         nc.vector.memset(tab_planes[:], 0)
         nc.vector.memset(warm[:], 0.0)
         nc.scalar.activation(warm_out[:], warm[:], ACT.Sigmoid)
@@ -50,66 +51,92 @@ def tile_list_hwayt_dl_siluP_kernel(
                 tab_scales[:, 4 * q : 4 * q + 4, :].bitcast(I32).rearrange("a r c -> r a c"),
             )
 
-        def load_planes(scales, tag):
+        def load_planes(scales, tag, queue):
             planes = keep.tile([P, PASSES * N // 4], I32, name="w_planes", tag=tag, align_bytes=64)
             nc.vector.memset(planes[:], 0)
             for q in range(4):
-                nc.scalar.dma_start(
+                queue.dma_start(
                     planes[32 * q : 32 * q + 4, :].rearrange("r (a c) -> r a c", a=PASSES),
                     scales[:, 4 * q : 4 * q + 4, :].bitcast(I32).rearrange("a r c -> r a c"),
                 )
             return planes
 
-        w_planes = (load_planes(wg_scales, "r1"), load_planes(wh4_scales, "wh4_planes"))
+        def deal_planes(planes, name):
+            dealt = keep.tile([P, PASSES, N], U8, name=name, align_bytes=64)
+            nc.vector.tensor_copy(
+                dealt[:].rearrange("p a (t m) -> p a m t", t=PACK),
+                planes[:].bitcast(U8).rearrange("p (a m t) -> p a m t", a=PASSES, t=PACK),
+            )
+            return dealt
 
         wg_raw = keep.tile([P, PASSES, N], I32, name="wg_raw", tag="whd1", align_bytes=64)
         nc.sync.dma_start(wg_raw[:], wg_words.rearrange("a p n i -> p a (n i)").bitcast(I32))
-        wh4_raw = keep.tile([P, PASSES, N // 2], I32, name="wh4_raw", tag="r0", align_bytes=64)
-        nc.sync.dma_start(wh4_raw[:], wh4_words.rearrange("a p c -> p a c").bitcast(I32))
+
+        def load_whd(a):
+            raw = keep.tile([P, PACK, N], F32, name="whd_raw%d" % a, tag="whd%d" % a, align_bytes=64)
+            nc.sync.dma_start(raw[:], whd[a * 512 : (a + 1) * 512, :].rearrange("(p i) n -> p i n", i=PACK))
+            return raw
+
+        whd_raw = [load_whd(0)]
         tab = keep.tile([P, T], I32, name="tab", tag="tab", align_bytes=64)
         nc.sync.dma_start(tab[:], tab_words[0].rearrange("p c i -> p (c i)").bitcast(I32))
+        wg_planes = load_planes(wg_scales, "r2", nc.scalar)
+        wg_dealt = keep.tile([P, PASSES, N], I32, name="wg_dealt", align_bytes=64)
+        nc.vector.tensor_copy(
+            wg_dealt[:].rearrange("p a (t m) -> p a m t", t=PACK),
+            wg_raw[:].rearrange("p a (m t) -> p a m t", t=PACK),
+        )
+        whd_raw.append(load_whd(1))
+        neg_bias = keep.tile([P, PACK], F32, name="neg_bias")
+        nc.vector.tensor_scalar(neg_bias[:], bias[:], -1.0, None, ALU.mult)
+        wh4_planes = load_planes(wh4_scales, "wh4_planes", nc.scalar)
+        wh4_raw = keep.tile([P, PASSES, N // 2], I32, name="wh4_raw")
+        nc.sync.dma_start(wh4_raw[:], wh4_words.rearrange("a p c -> p a c").bitcast(I32))
+
+        whd_codes = keep.tile([P, PASSES, N], U32, name="whd_codes", align_bytes=64)
+        whd_scales = keep.tile([P, PASSES, N], U8, name="whd_scales", align_bytes=64)
+
+        def round_whd(a):
+            grouped = keep.tile([P, N * PACK], BF16, name="whd_grouped%d" % a, tag=("grouped0", "r3")[a], align_bytes=64)
+            nc.scalar.copy(
+                grouped[:].rearrange("p (t m i) -> p m i t", t=PACK, i=PACK),
+                whd_raw[a][:].rearrange("p i (m t) -> p m i t", t=PACK),
+            )
+            return grouped
+
+        def quantise_whd(a):
+            nc.vector.quantize_mx(
+                out=whd_codes[:, a, :].bitcast(FP8X4), scales=whd_scales[:, a, :], in_=whd_grouped[a][:]
+            )
+
+        whd_grouped = [round_whd(a) for a in range(PASSES)]
         v_scales = []
         for a in range(PASSES):
             got = keep.tile([P, J], U8, name="v_scales%d" % a, align_bytes=64)
             nc.vector.tensor_copy(got[:], tab_planes[:].bitcast(U8)[:, a * T : (a + 1) * T].indirect(offsets[:]))
             v_scales.append(got)
 
-        wg_dealt = keep.tile([P, PASSES, N], I32, name="wg_dealt", align_bytes=64)
-        nc.vector.tensor_copy(
-            wg_dealt[:].rearrange("p a (t m) -> p a m t", t=PACK),
-            wg_raw[:].rearrange("p a (m t) -> p a m t", t=PACK),
-        )
-        wh4_dealt = keep.tile([P, PASSES, N], U16, name="wh4_dealt", align_bytes=64)
-        nc.vector.tensor_copy(
-            wh4_dealt[:].rearrange("p a (t m) -> p a m t", t=PACK),
-            wh4_raw[:].bitcast(U16).rearrange("p a (m t) -> p a m t", t=PACK),
-        )
-        w_scales = []
-        for w, planes in enumerate(w_planes):
-            dealt = keep.tile([P, PASSES, N], U8, name="w_scales%d" % w, align_bytes=64)
-            nc.vector.tensor_copy(
-                dealt[:].rearrange("p a (t m) -> p a m t", t=PACK),
-                planes[:].bitcast(U8).rearrange("p (a m t) -> p a m t", a=PASSES, t=PACK),
-            )
-            w_scales.append(dealt)
-        neg_bias = keep.tile([P, PACK], F32, name="neg_bias")
-        nc.vector.tensor_scalar(neg_bias[:], bias[:], -1.0, None, ALU.mult)
 
         v_words = []
         for h in range(HALVES):
-            pairs = keep.tile([P, BANK], I32, name="pairs%d" % h, tag=("r3", "pairs1")[h], align_bytes=64)
+            pairs = keep.tile([P, BANK], I32, name="pairs%d" % h, tag="r%d" % (1 + h), align_bytes=64)
             nc.vector.tensor_copy(
                 pairs[:].bitcast(U32), tab[:].bitcast(U32).indirect(offsets[:, h * 32 : (h + 1) * 32])
             )
             parted = keep.tile([P, PASSES, BANK], U16, name="parted%d" % h, align_bytes=64)
             nc.vector.tensor_copy(parted[:], pairs[:].bitcast(U16).rearrange("p (j d) -> p d j", d=PASSES))
             v_words.append(parted)
+            if h == 0:
+                w_scales = [deal_planes(wg_planes, "wg_dealt_scales")]
+        quantise_whd(0)
+        wh4_dealt = keep.tile([P, PASSES, N], U16, name="wh4_dealt", align_bytes=64)
+        nc.vector.tensor_copy(
+            wh4_dealt[:].rearrange("p a (t m) -> p a m t", t=PACK),
+            wh4_raw[:].bitcast(U16).rearrange("p a (m t) -> p a m t", t=PACK),
+        )
+        w_scales.append(deal_planes(wh4_planes, "wh4_dealt_scales"))
+        quantise_whd(1)
 
-        whd_raw = []
-        for a in range(PASSES):
-            raw = keep.tile([P, PACK, N], F32, name="whd_raw%d" % a, tag="whd%d" % a, align_bytes=64)
-            nc.sync.dma_start(raw[:], whd[a * 512 : (a + 1) * 512, :].rearrange("(p i) n -> p i n", i=PACK))
-            whd_raw.append(raw)
         r_rows = rT.rearrange("(p t) c -> p t c", t=PACK)
         r_tiles = []
         for t in range(PACK):
@@ -123,20 +150,10 @@ def tile_list_hwayt_dl_siluP_kernel(
                 rhs_scale=v_scales[a][:, h * BANK : (h + 1) * BANK],
             )
 
-        whd_codes = keep.tile([P, PASSES, N], U32, name="whd_codes", align_bytes=64)
-        whd_scales = keep.tile([P, PASSES, N], U8, name="whd_scales", align_bytes=64)
-        for a in range(PASSES):
-            grouped = keep.tile([P, N * PACK], BF16, name="whd_grouped%d" % a, align_bytes=64)
-            nc.scalar.copy(
-                grouped[:].rearrange("p (t m i) -> p m i t", t=PACK, i=PACK),
-                whd_raw[a][:].rearrange("p i (m t) -> p m i t", t=PACK),
-            )
-            nc.vector.quantize_mx(out=whd_codes[:, a, :].bitcast(FP8X4), scales=whd_scales[:, a, :], in_=grouped[:])
-
-        carry = keep.tile([P, PACK, J], F32, name="carry")
+        carry = [keep.tile([P, J], F32, name="carry%d" % t) for t in range(PACK)]
         for h in range(HALVES):
             for t in range(PACK):
-                ga = psum.tile([P, BANK], F32, name="bank%d" % (2 * t + h))
+                ga = psum.tile([P, BANK], F32, name="ga", bufs=5)
                 cols = slice(t * P, (t + 1) * P)
                 for a in range(PASSES):
                     nc.tensor.matmul_mx(
@@ -148,14 +165,14 @@ def tile_list_hwayt_dl_siluP_kernel(
                         **moving(a, h),
                     )
                 nc.scalar.activation(
-                    carry[:, t, h * BANK : (h + 1) * BANK], ga[:], ACT.Sigmoid, bias=neg_bias[:, t : t + 1], scale=-1.0
+                    carry[t][:, h * BANK : (h + 1) * BANK], ga[:], ACT.Sigmoid, bias=neg_bias[:, t : t + 1], scale=-1.0
                 )
 
-        made = keep.tile([P, PACK, J], F32, name="made")
+        made = [keep.tile([P, J], F32, name="made%d" % t) for t in range(PACK)]
         for t in range(PACK):
             cols = slice(t * P, (t + 1) * P)
             for h in range(HALVES):
-                ha = psum.tile([P, BANK], F32, name="bank%d" % (2 * t + h))
+                ha = psum.tile([P, BANK], F32, name="ha", bufs=3)
                 for a in range(PASSES):
                     nc.tensor.matmul_mx(
                         out=ha[:],
@@ -174,51 +191,62 @@ def tile_list_hwayt_dl_siluP_kernel(
                         stop=(a == PASSES - 1),
                         **moving(a, h),
                     )
-                nc.scalar.activation(made[:, t, h * BANK : (h + 1) * BANK], ha[:], ACT.Silu)
+                nc.scalar.activation(made[t][:, h * BANK : (h + 1) * BANK], ha[:], ACT.Silu)
 
         y = keep.tile([P, PACK, J], F32, name="y")
         y_rows = out_0.rearrange("(p t) j -> p t j", t=PACK)
-        for t in range(PACK):
-            nc.vector.scalar_tensor_tensor(
-                made[:, t, :], carry[:, t, :], 1.0, made[:, t, :], ALU.subtract, ALU.mult
-            )
-            if t < PACK - 1:
-                nc.vector.tensor_tensor(y[:, t, :], r_tiles[t][:].indirect(offsets[:]), carry[:, t, :], ALU.mult)
-                nc.vector.tensor_tensor(y[:, t, :], y[:, t, :], made[:, t, :], ALU.subtract)
-                nc.sync.dma_start(y_rows[:, t, :], y[:, t, :])
 
-        y_round = keep.tile([P, J * PACK], BF16, name="y_round", align_bytes=64)
+        def gate_made(t):
+            nc.vector.scalar_tensor_tensor(made[t][:, :], carry[t][:, :], 1.0, made[t][:, :], ALU.subtract, ALU.mult)
+
+        for t in range(PACK - 1):
+            kept = keep.tile([P, J], F32, name="kept", bufs=2)
+            nc.vector.tensor_tensor(kept[:], r_tiles[t][:].indirect(offsets[:]), carry[t][:, :], ALU.mult)
+            gate_made(t)
+            nc.vector.tensor_tensor(y[:, t, :], kept[:], made[t][:, :], ALU.subtract)
+            nc.sync.dma_start(y_rows[:, t, :], y[:, t, :])
+        t = PACK - 1
+        gate_made(t)
+        kept = keep.tile([P, J], F32, name="kept", bufs=2)
+
         y_codes = keep.tile([P, J], I32, name="y_codes", align_bytes=64)
         y_scales = keep.tile([P, J], U8, name="y_scales", align_bytes=64)
         code_rows = out_1[0].rearrange("p j i -> p (j i)").bitcast(I32)
-        t = PACK - 1
-        j0 = 0
-        pending = None
-
-        def finish(js):
-            nc.vector.quantize_mx(
-                out=y_codes[:, js].bitcast(FP8X4),
-                scales=y_scales[:, js],
-                in_=y_round[:, js.start * PACK : js.stop * PACK],
-            )
-            nc.sync.dma_start(code_rows[:, js], y_codes[:, js])
-
+        chunks = []
         for width in LAST_CHUNKS:
-            js = slice(j0, j0 + width)
+            j0 = chunks[-1].stop if chunks else 0
+            chunks.append(slice(j0, j0 + width))
+        rounded = {}
+
+        def look_up(js):
             nc.vector.tensor_tensor(
-                y[:, t, js], r_tiles[t][:].indirect(offsets[:, j0 // 16 : (j0 + width) // 16]), carry[:, t, js], ALU.mult
+                kept[:, js], r_tiles[t][:].indirect(offsets[:, js.start // 16 : js.stop // 16]), carry[t][:, js], ALU.mult
             )
-            nc.vector.tensor_tensor(y[:, t, js], y[:, t, js], made[:, t, js], ALU.subtract)
-            nc.sync.dma_start(y_rows[:, t, js], y[:, t, js])
+
+        def combine(c, js):
+            nc.vector.tensor_tensor(y[:, t, js], kept[:, js], made[t][:, js], ALU.subtract)
+            rounded[c] = keep.tile([P, (js.stop - js.start) * PACK], BF16, name="y_round%d" % c, align_bytes=64)
             nc.scalar.copy(
-                y_round[:, j0 * PACK : (j0 + width) * PACK].rearrange("p (c i t) -> p c t i", i=4, t=PACK),
+                rounded[c][:].rearrange("p (c i t) -> p c t i", i=4, t=PACK),
                 y[:, :, js].rearrange("p t (c i) -> p c t i", i=4),
             )
-            if pending is not None:
-                finish(pending)
-            pending = js
-            j0 = j0 + width
-        finish(pending)
+            if js.stop in STORE_FROM:
+                ss = slice(STORE_FROM[js.stop], js.stop)
+                nc.sync.dma_start(y_rows[:, t, ss], y[:, t, ss])
+
+        def quantise(c, js):
+            nc.vector.quantize_mx(out=y_codes[:, js].bitcast(FP8X4), scales=y_scales[:, js], in_=rounded[c][:])
+            if js.stop in STORE_FROM:
+                ss = slice(STORE_FROM[js.stop], js.stop)
+                nc.sync.dma_start(code_rows[:, ss], y_codes[:, ss])
+
+        for c in range(len(chunks) + 2):
+            if c < len(chunks):
+                look_up(chunks[c])
+            if c >= 2:
+                quantise(c - 2, chunks[c - 2])
+            if 1 <= c <= len(chunks):
+                combine(c - 1, chunks[c - 1])
         for q in range(4):
             queue = nc.scalar if q % 2 else nc.sync
             queue.dma_start(

@@ -36,10 +36,10 @@ def tile_list_hwayt_dl_siluP_kernel(
         offsets = keep.tile([P, J // 16], U16, name="offsets")
         nc.sync.dma_start(offsets[:], offs)
 
-        bias = keep.tile([P, PACK], F32, name="bias", tag="wh4_planes", align_bytes=64)
+        bias = keep.tile([P, PACK], F32, name="bias")
         nc.scalar.dma_start(bias[:], bg.rearrange("(p t) -> p t", t=PACK))
         warm = keep.tile([P, 1], F32, name="warm", tag="tab", align_bytes=64)
-        warm_out = keep.tile([P, 1], F32, name="warm_out", tag="r2", align_bytes=64)
+        warm_out = keep.tile([P, 1], F32, name="warm_out", tag="r1", align_bytes=64)
 
         tab_planes = keep.tile([P, PASSES * T // 4], I32, name="tab_planes", tag="r0", align_bytes=64)
         nc.vector.memset(tab_planes[:], 0)
@@ -64,8 +64,8 @@ def tile_list_hwayt_dl_siluP_kernel(
         def deal_planes(planes, name):
             dealt = keep.tile([P, PASSES, N], U8, name=name, align_bytes=64)
             nc.vector.tensor_copy(
-                dealt[:].rearrange("p a (t m) -> p a m t", t=PACK),
-                planes[:].bitcast(U8).rearrange("p (a m t) -> p a m t", a=PASSES, t=PACK),
+                dealt[:].rearrange("p a (t c i) -> p a c t i", t=PACK, i=16),
+                planes[:].bitcast(U8).rearrange("p (a c i t) -> p a c t i", a=PASSES, t=PACK, i=16),
             )
             return dealt
 
@@ -80,16 +80,15 @@ def tile_list_hwayt_dl_siluP_kernel(
         whd_raw = [load_whd(0)]
         tab = keep.tile([P, T], I32, name="tab", tag="tab", align_bytes=64)
         nc.sync.dma_start(tab[:], tab_words[0].rearrange("p c i -> p (c i)").bitcast(I32))
-        wg_planes = load_planes(wg_scales, "r2", nc.scalar)
+        wg_planes = load_planes(wg_scales, "r1", nc.scalar)
         wg_dealt = keep.tile([P, PASSES, N], I32, name="wg_dealt", align_bytes=64)
         nc.vector.tensor_copy(
-            wg_dealt[:].rearrange("p a (t m) -> p a m t", t=PACK),
-            wg_raw[:].rearrange("p a (m t) -> p a m t", t=PACK),
+            wg_dealt[:].rearrange("p a (t c i) -> p a c t i", t=PACK, i=4),
+            wg_raw[:].rearrange("p a (c i t) -> p a c t i", t=PACK, i=4),
         )
         whd_raw.append(load_whd(1))
         neg_bias = keep.tile([P, PACK], F32, name="neg_bias")
         nc.vector.tensor_scalar(neg_bias[:], bias[:], -1.0, None, ALU.mult)
-        wh4_planes = load_planes(wh4_scales, "wh4_planes", nc.scalar)
         wh4_raw = keep.tile([P, PASSES, N // 2], I32, name="wh4_raw")
         nc.sync.dma_start(wh4_raw[:], wh4_words.rearrange("a p c -> p a c").bitcast(I32))
 
@@ -99,8 +98,8 @@ def tile_list_hwayt_dl_siluP_kernel(
         def round_whd(a):
             grouped = keep.tile([P, N * PACK], BF16, name="whd_grouped%d" % a, tag=("grouped0", "r3")[a], align_bytes=64)
             nc.scalar.copy(
-                grouped[:].rearrange("p (t m i) -> p m i t", t=PACK, i=PACK),
-                whd_raw[a][:].rearrange("p i (m t) -> p m i t", t=PACK),
+                grouped[:].rearrange("p (t m i) -> p m t i", t=PACK, i=PACK),
+                whd_raw[a][:].rearrange("p i (m t) -> p m t i", t=PACK),
             )
             return grouped
 
@@ -119,7 +118,7 @@ def tile_list_hwayt_dl_siluP_kernel(
 
         v_words = []
         for h in range(HALVES):
-            pairs = keep.tile([P, BANK], I32, name="pairs%d" % h, tag="r%d" % (1 + h), align_bytes=64)
+            pairs = keep.tile([P, BANK], I32, name="pairs%d" % h, tag="r%d" % (2 - h), align_bytes=64)
             nc.vector.tensor_copy(
                 pairs[:].bitcast(U32), tab[:].bitcast(U32).indirect(offsets[:, h * 32 : (h + 1) * 32])
             )
@@ -128,14 +127,15 @@ def tile_list_hwayt_dl_siluP_kernel(
             v_words.append(parted)
             if h == 0:
                 w_scales = [deal_planes(wg_planes, "wg_dealt_scales")]
+                wh4_planes = load_planes(wh4_scales, "r2", nc.scalar)
         quantise_whd(0)
         wh4_dealt = keep.tile([P, PASSES, N], U16, name="wh4_dealt", align_bytes=64)
         nc.vector.tensor_copy(
-            wh4_dealt[:].rearrange("p a (t m) -> p a m t", t=PACK),
-            wh4_raw[:].bitcast(U16).rearrange("p a (m t) -> p a m t", t=PACK),
+            wh4_dealt[:].rearrange("p a (t c i) -> p a c t i", t=PACK, i=8),
+            wh4_raw[:].bitcast(U16).rearrange("p a (c i t) -> p a c t i", t=PACK, i=8),
         )
-        w_scales.append(deal_planes(wh4_planes, "wh4_dealt_scales"))
         quantise_whd(1)
+        w_scales.append(deal_planes(wh4_planes, "wh4_dealt_scales"))
 
         r_rows = rT.rearrange("(p t) c -> p t c", t=PACK)
         r_tiles = []

@@ -39,16 +39,16 @@ def tile_list_hwayt_dl_siluP_kernel(
         bias = keep.tile([P, PACK], F32, name="bias")
         nc.scalar.dma_start(bias[:], bg.rearrange("(p t) -> p t", t=PACK))
         warm = keep.tile([P, 1], F32, name="warm", tag="tab", align_bytes=64)
-        warm_out = keep.tile([P, 1], F32, name="warm_out", tag="r1", align_bytes=64)
+        warm_out = keep.tile([P, 1], F32, name="warm_out")
 
-        tab_planes = keep.tile([P, PASSES * T // 4], I32, name="tab_planes", tag="r0", align_bytes=64)
+        tab_planes = keep.tile([P, T // 4], I32, name="tab_planes", tag="whd", align_bytes=64)
         nc.vector.memset(tab_planes[:], 0)
         nc.vector.memset(warm[:], 0.0)
         nc.scalar.activation(warm_out[:], warm[:], ACT.Sigmoid)
         for q in range(4):
             nc.sync.dma_start(
-                tab_planes[32 * q : 32 * q + 4, :].rearrange("r (a c) -> r a c", a=PASSES),
-                tab_scales[:, 4 * q : 4 * q + 4, :].bitcast(I32).rearrange("a r c -> r a c"),
+                tab_planes[32 * q : 32 * q + 4 * PASSES, :],
+                tab_scales[:, 4 * q : 4 * q + 4, :].bitcast(I32),
             )
 
         def load_planes(scales, tag, queue):
@@ -69,15 +69,11 @@ def tile_list_hwayt_dl_siluP_kernel(
             )
             return dealt
 
-        wg_raw = keep.tile([P, PASSES, N], I32, name="wg_raw", tag="whd1", align_bytes=64)
+        wg_raw = keep.tile([P, PASSES, N], I32, name="wg_raw", tag="wh4_planes", align_bytes=64)
         nc.sync.dma_start(wg_raw[:], wg_words.rearrange("a p n i -> p a (n i)").bitcast(I32))
 
-        def load_whd(a):
-            raw = keep.tile([P, PACK, N], F32, name="whd_raw%d" % a, tag="whd%d" % a, align_bytes=64)
-            nc.sync.dma_start(raw[:], whd[a * 512 : (a + 1) * 512, :].rearrange("(p i) n -> p i n", i=PACK))
-            return raw
-
-        whd_raw = [load_whd(0)]
+        wh4_raw = keep.tile([P, PASSES, N // 2], I32, name="wh4_raw")
+        nc.sync.dma_start(wh4_raw[:], wh4_words.rearrange("a p c -> p a c").bitcast(I32))
         tab = keep.tile([P, T], I32, name="tab", tag="tab", align_bytes=64)
         nc.sync.dma_start(tab[:], tab_words[0].rearrange("p c i -> p (c i)").bitcast(I32))
         wg_planes = load_planes(wg_scales, "r1", nc.scalar)
@@ -86,20 +82,18 @@ def tile_list_hwayt_dl_siluP_kernel(
             wg_dealt[:].rearrange("p a (t c i) -> p a c t i", t=PACK, i=4),
             wg_raw[:].rearrange("p a (c i t) -> p a c t i", t=PACK, i=4),
         )
-        whd_raw.append(load_whd(1))
+        wh4_planes = load_planes(wh4_scales, "wh4_planes", nc.scalar)
         neg_bias = keep.tile([P, PACK], F32, name="neg_bias")
         nc.vector.tensor_scalar(neg_bias[:], bias[:], -1.0, None, ALU.mult)
-        wh4_raw = keep.tile([P, PASSES, N // 2], I32, name="wh4_raw")
-        nc.sync.dma_start(wh4_raw[:], wh4_words.rearrange("a p c -> p a c").bitcast(I32))
 
         whd_codes = keep.tile([P, PASSES, N], U32, name="whd_codes", align_bytes=64)
         whd_scales = keep.tile([P, PASSES, N], U8, name="whd_scales", align_bytes=64)
 
         def round_whd(a):
-            grouped = keep.tile([P, N * PACK], BF16, name="whd_grouped%d" % a, tag=("grouped0", "r3")[a], align_bytes=64)
-            nc.scalar.copy(
+            grouped = keep.tile([P, N * PACK], BF16, name="whd_grouped%d" % a, tag="r%d" % (2 + a), align_bytes=64)
+            (nc.scalar.copy, nc.vector.tensor_copy)[a](
                 grouped[:].rearrange("p (t m i) -> p m t i", t=PACK, i=PACK),
-                whd_raw[a][:].rearrange("p i (m t) -> p m t i", t=PACK),
+                whd_raw[:, a * PACK * N : (a + 1) * PACK * N].rearrange("p (i m t) -> p m t i", i=PACK, t=PACK),
             )
             return grouped
 
@@ -108,17 +102,33 @@ def tile_list_hwayt_dl_siluP_kernel(
                 out=whd_codes[:, a, :].bitcast(FP8X4), scales=whd_scales[:, a, :], in_=whd_grouped[a][:]
             )
 
-        whd_grouped = [round_whd(a) for a in range(PASSES)]
-        v_scales = []
+        picked_planes = keep.tile([P, J], U8, name="picked_planes", align_bytes=64)
+        nc.vector.tensor_copy(picked_planes[:], tab_planes[:].bitcast(U8).indirect(offsets[:]))
+        second_plane = keep.tile([P, J], U8, name="second_plane", align_bytes=64)
+        nc.gpsimd.memset(second_plane[:].bitcast(I32), 0)
+        for q in range(4):
+            nc.scalar.dma_start(
+                second_plane[32 * q : 32 * q + 4, :].bitcast(I32),
+                picked_planes[32 * q + 4 : 32 * q + 8, :].bitcast(I32),
+            )
+        v_scales = (picked_planes, second_plane)
+
+        whd_raw = keep.tile([P, PASSES * PACK * N], F32, name="whd_raw", tag="whd", align_bytes=64)
         for a in range(PASSES):
-            got = keep.tile([P, J], U8, name="v_scales%d" % a, align_bytes=64)
-            nc.vector.tensor_copy(got[:], tab_planes[:].bitcast(U8)[:, a * T : (a + 1) * T].indirect(offsets[:]))
-            v_scales.append(got)
+            nc.sync.dma_start(
+                whd_raw[:, a * PACK * N : (a + 1) * PACK * N],
+                whd[a * 512 : (a + 1) * 512, :].rearrange("(p i) n -> p (i n)", i=PACK),
+            )
+        whd_grouped = [round_whd(0)]
 
-
+        wh4_dealt = keep.tile([P, PASSES, N], U16, name="wh4_dealt", align_bytes=64)
+        nc.vector.tensor_copy(
+            wh4_dealt[:].rearrange("p a (t c i) -> p a c t i", t=PACK, i=8),
+            wh4_raw[:].bitcast(U16).rearrange("p a (c i t) -> p a c t i", t=PACK, i=8),
+        )
         v_words = []
         for h in range(HALVES):
-            pairs = keep.tile([P, BANK], I32, name="pairs%d" % h, tag="r%d" % (2 - h), align_bytes=64)
+            pairs = keep.tile([P, BANK], I32, name="pairs%d" % h, tag="r%d" % h, align_bytes=64)
             nc.vector.tensor_copy(
                 pairs[:].bitcast(U32), tab[:].bitcast(U32).indirect(offsets[:, h * 32 : (h + 1) * 32])
             )
@@ -127,15 +137,10 @@ def tile_list_hwayt_dl_siluP_kernel(
             v_words.append(parted)
             if h == 0:
                 w_scales = [deal_planes(wg_planes, "wg_dealt_scales")]
-                wh4_planes = load_planes(wh4_scales, "r2", nc.scalar)
-        quantise_whd(0)
-        wh4_dealt = keep.tile([P, PASSES, N], U16, name="wh4_dealt", align_bytes=64)
-        nc.vector.tensor_copy(
-            wh4_dealt[:].rearrange("p a (t c i) -> p a c t i", t=PACK, i=8),
-            wh4_raw[:].bitcast(U16).rearrange("p a (c i t) -> p a c t i", t=PACK, i=8),
-        )
-        quantise_whd(1)
         w_scales.append(deal_planes(wh4_planes, "wh4_dealt_scales"))
+        whd_grouped.append(round_whd(1))
+        quantise_whd(0)
+        quantise_whd(1)
 
         r_rows = rT.rearrange("(p t) c -> p t c", t=PACK)
         r_tiles = []

@@ -21,8 +21,10 @@ PACK = 4
 PASSES = K // (P * PACK)
 BANK = 512
 HALVES = J // BANK
-LAST_CHUNKS = (256, 256, 256, 128, 128)
-STORE_FROM = {512: 0, 768: 512, 1024: 768}
+ROWS_AT = 96
+PLANE = 2 * N + J
+LAST_CHUNKS = (128, 256, 256, 256, 128)
+STORE_FROM = {384: 0, 896: 384, 1024: 896}
 
 
 def tile_list_hwayt_dl_siluP_kernel(
@@ -36,96 +38,60 @@ def tile_list_hwayt_dl_siluP_kernel(
         offsets = keep.tile([P, J // 16], U16, name="offsets")
         nc.sync.dma_start(offsets[:], offs)
 
+        tab_rows = keep.tile([P, T // 4], I32, name="tab_rows", align_bytes=64)
+        nc.vector.memset(tab_rows[0:ROWS_AT, :], 0)
+        nc.sync.dma_start(tab_rows[ROWS_AT:P, :], tab_scales.bitcast(I32).rearrange("a q c -> q a c"))
+        w_rows = keep.tile([P, 2, N // 4], I32, name="w_rows", align_bytes=64)
+        nc.vector.memset(w_rows[0:ROWS_AT, :, :], 0)
+        for w, scales in enumerate((wg_scales, wh4_scales)):
+            nc.sync.dma_start(w_rows[ROWS_AT:P, w, :], scales.bitcast(I32).rearrange("a q c -> q a c"))
+        planes = keep.tile([P, PASSES * PLANE // 4], I32, name="planes", align_bytes=64)
+        nc.vector.memset(planes[:], 0)
+
         bias = keep.tile([P, PACK], F32, name="bias")
         nc.scalar.dma_start(bias[:], bg.rearrange("(p t) -> p t", t=PACK))
-        warm = keep.tile([P, 1], F32, name="warm", tag="tab", align_bytes=64)
+        warm = keep.tile([P, 1], F32, name="warm")
         warm_out = keep.tile([P, 1], F32, name="warm_out")
+        nc.gpsimd.memset(warm[:], 0.0)
+        nc.scalar.activation(warm_out[:], warm[:], ACT.Silu)
 
-        tab_planes = keep.tile([P, T // 4], I32, name="tab_planes", tag="whd", align_bytes=64)
-        nc.vector.memset(tab_planes[:], 0)
-        nc.vector.memset(warm[:], 0.0)
-        nc.scalar.activation(warm_out[:], warm[:], ACT.Sigmoid)
-        for q in range(4):
-            nc.sync.dma_start(
-                tab_planes[32 * q : 32 * q + 4 * PASSES, :],
-                tab_scales[:, 4 * q : 4 * q + 4, :].bitcast(I32),
-            )
-
-        def load_planes(scales, tag, queue):
-            planes = keep.tile([P, PASSES * N // 4], I32, name="w_planes", tag=tag, align_bytes=64)
-            nc.vector.memset(planes[:], 0)
-            for q in range(4):
-                queue.dma_start(
-                    planes[32 * q : 32 * q + 4, :].rearrange("r (a c) -> r a c", a=PASSES),
-                    scales[:, 4 * q : 4 * q + 4, :].bitcast(I32).rearrange("a r c -> r a c"),
-                )
-            return planes
-
-        def deal_planes(planes, name):
-            dealt = keep.tile([P, PASSES, N], U8, name=name, align_bytes=64)
-            nc.vector.tensor_copy(
-                dealt[:].rearrange("p a (t c i) -> p a c t i", t=PACK, i=16),
-                planes[:].bitcast(U8).rearrange("p (a c i t) -> p a c t i", a=PASSES, t=PACK, i=16),
-            )
-            return dealt
-
-        wg_raw = keep.tile([P, PASSES, N], I32, name="wg_raw", tag="wh4_planes", align_bytes=64)
+        wg_raw = keep.tile([P, PASSES, N], I32, name="wg_raw", align_bytes=64)
         nc.sync.dma_start(wg_raw[:], wg_words.rearrange("a p n i -> p a (n i)").bitcast(I32))
-
         wh4_raw = keep.tile([P, PASSES, N // 2], I32, name="wh4_raw")
         nc.sync.dma_start(wh4_raw[:], wh4_words.rearrange("a p c -> p a c").bitcast(I32))
-        tab = keep.tile([P, T], I32, name="tab", tag="tab", align_bytes=64)
+        tab = keep.tile([P, T], I32, name="tab", align_bytes=64)
         nc.sync.dma_start(tab[:], tab_words[0].rearrange("p c i -> p (c i)").bitcast(I32))
-        wg_planes = load_planes(wg_scales, "r1", nc.scalar)
+
+        picked = keep.tile([P, J], U8, name="picked", tag="r2", align_bytes=64)
+        nc.vector.tensor_copy(picked[:], tab_rows[:].bitcast(U8).indirect(offsets[:]))
+        staged = keep.tile([P, PLANE // 4], I32, name="staged", tag="r3", align_bytes=64)
+        nc.vector.tensor_copy(
+            staged[:, 0 : 2 * N // 4].bitcast(U8).rearrange("p (w t c i) -> p w c t i", w=2, t=PACK, i=16),
+            w_rows[:].bitcast(U8).rearrange("p w (c i t) -> p w c t i", t=PACK, i=16),
+        )
+        nc.vector.tensor_copy(staged[:, 2 * N // 4 :], picked[:].bitcast(I32))
+        for q in range(4):
+            nc.sync.dma_start(planes[32 * q : 32 * q + 4, :], staged[ROWS_AT + 8 * q : ROWS_AT + 8 * q + 8, :])
+        plane_bytes = planes[:].bitcast(U8)
+        whd_raw = []
+        for a in range(PASSES):
+            raw = keep.tile([P, PACK * N], F32, name="whd_raw%d" % a, tag="r%d" % (2 + a), align_bytes=64)
+            nc.sync.dma_start(raw[:], whd[a * 512 : (a + 1) * 512, :].rearrange("(p i) n -> p (i n)", i=PACK))
+            whd_raw.append(raw)
+
         wg_dealt = keep.tile([P, PASSES, N], I32, name="wg_dealt", align_bytes=64)
         nc.vector.tensor_copy(
             wg_dealt[:].rearrange("p a (t c i) -> p a c t i", t=PACK, i=4),
             wg_raw[:].rearrange("p a (c i t) -> p a c t i", t=PACK, i=4),
         )
-        wh4_planes = load_planes(wh4_scales, "wh4_planes", nc.scalar)
-        neg_bias = keep.tile([P, PACK], F32, name="neg_bias")
-        nc.vector.tensor_scalar(neg_bias[:], bias[:], -1.0, None, ALU.mult)
-
-        whd_codes = keep.tile([P, PASSES, N], U32, name="whd_codes", align_bytes=64)
-        whd_scales = keep.tile([P, PASSES, N], U8, name="whd_scales", align_bytes=64)
-
-        def round_whd(a):
-            grouped = keep.tile([P, N * PACK], BF16, name="whd_grouped%d" % a, tag="r%d" % (2 + a), align_bytes=64)
-            (nc.scalar.copy, nc.vector.tensor_copy)[a](
-                grouped[:].rearrange("p (t m i) -> p m t i", t=PACK, i=PACK),
-                whd_raw[:, a * PACK * N : (a + 1) * PACK * N].rearrange("p (i m t) -> p m t i", i=PACK, t=PACK),
-            )
-            return grouped
-
-        def quantise_whd(a):
-            nc.vector.quantize_mx(
-                out=whd_codes[:, a, :].bitcast(FP8X4), scales=whd_scales[:, a, :], in_=whd_grouped[a][:]
-            )
-
-        picked_planes = keep.tile([P, J], U8, name="picked_planes", align_bytes=64)
-        nc.vector.tensor_copy(picked_planes[:], tab_planes[:].bitcast(U8).indirect(offsets[:]))
-        second_plane = keep.tile([P, J], U8, name="second_plane", align_bytes=64)
-        nc.gpsimd.memset(second_plane[:].bitcast(I32), 0)
-        for q in range(4):
-            nc.scalar.dma_start(
-                second_plane[32 * q : 32 * q + 4, :].bitcast(I32),
-                picked_planes[32 * q + 4 : 32 * q + 8, :].bitcast(I32),
-            )
-        v_scales = (picked_planes, second_plane)
-
-        whd_raw = keep.tile([P, PASSES * PACK * N], F32, name="whd_raw", tag="whd", align_bytes=64)
-        for a in range(PASSES):
-            nc.sync.dma_start(
-                whd_raw[:, a * PACK * N : (a + 1) * PACK * N],
-                whd[a * 512 : (a + 1) * 512, :].rearrange("(p i) n -> p (i n)", i=PACK),
-            )
-        whd_grouped = [round_whd(0)]
-
         wh4_dealt = keep.tile([P, PASSES, N], U16, name="wh4_dealt", align_bytes=64)
         nc.vector.tensor_copy(
             wh4_dealt[:].rearrange("p a (t c i) -> p a c t i", t=PACK, i=8),
             wh4_raw[:].bitcast(U16).rearrange("p a (c i t) -> p a c t i", t=PACK, i=8),
         )
+        half_bias = keep.tile([P, PACK], F32, name="half_bias")
+        nc.vector.tensor_scalar(half_bias[:], bias[:], 0.5, None, ALU.mult)
+
         v_words = []
         for h in range(HALVES):
             pairs = keep.tile([P, BANK], I32, name="pairs%d" % h, tag="r%d" % h, align_bytes=64)
@@ -135,12 +101,21 @@ def tile_list_hwayt_dl_siluP_kernel(
             parted = keep.tile([P, PASSES, BANK], U16, name="parted%d" % h, align_bytes=64)
             nc.vector.tensor_copy(parted[:], pairs[:].bitcast(U16).rearrange("p (j d) -> p d j", d=PASSES))
             v_words.append(parted)
-            if h == 0:
-                w_scales = [deal_planes(wg_planes, "wg_dealt_scales")]
-        w_scales.append(deal_planes(wh4_planes, "wh4_dealt_scales"))
-        whd_grouped.append(round_whd(1))
-        quantise_whd(0)
-        quantise_whd(1)
+
+        whd_grouped, whd_codes, whd_scales = [], [], []
+        for a in range(PASSES):
+            grouped = keep.tile([P, N * PACK], BF16, name="whd_grouped%d" % a, align_bytes=64)
+            nc.vector.tensor_copy(
+                grouped[:].rearrange("p (t m i) -> p m t i", t=PACK, i=PACK),
+                whd_raw[a][:].rearrange("p (i m t) -> p m t i", i=PACK, t=PACK),
+            )
+            whd_grouped.append(grouped)
+        for a in range(PASSES):
+            codes = keep.tile([P, N], U32, name="whd_codes%d" % a, align_bytes=64)
+            scale_bytes = keep.tile([P, N], U8, name="whd_scales%d" % a, align_bytes=64)
+            nc.vector.quantize_mx(out=codes[:].bitcast(FP8X4), scales=scale_bytes[:], in_=whd_grouped[a][:])
+            whd_codes.append(codes)
+            whd_scales.append(scale_bytes)
 
         r_rows = rT.rearrange("(p t) c -> p t c", t=PACK)
         r_tiles = []
@@ -150,69 +125,69 @@ def tile_list_hwayt_dl_siluP_kernel(
             r_tiles.append(r_tile)
 
         def moving(a, h):
-            return dict(
-                rhs=v_words[h][:, a, :].bitcast(U8).bitcast(FP4X4),
-                rhs_scale=v_scales[a][:, h * BANK : (h + 1) * BANK],
-            )
+            at = a * PLANE + 2 * N + h * BANK
+            return dict(rhs=v_words[h][:, a, :].bitcast(U8).bitcast(FP4X4), rhs_scale=plane_bytes[:, at : at + BANK])
 
-        carry = [keep.tile([P, J], F32, name="carry%d" % t) for t in range(PACK)]
-        for h in range(HALVES):
-            for t in range(PACK):
-                ga = psum.tile([P, BANK], F32, name="ga", bufs=5)
-                cols = slice(t * P, (t + 1) * P)
+        def w_plane(w, a, t):
+            at = a * PLANE + w * N + t * P
+            return plane_bytes[:, at : at + P]
+
+        lean = [keep.tile([P, J], F32, name="lean%d" % t) for t in range(PACK)]
+        made = [keep.tile([P, J], F32, name="made%d" % t) for t in range(PACK)]
+        for t in range(PACK):
+            cols = slice(t * P, (t + 1) * P)
+            for h in range(HALVES):
+                ga = psum.tile([P, BANK], F32, name="ga", tag="bank%d" % ((4 * t + h) % 6))
                 for a in range(PASSES):
                     nc.tensor.matmul_mx(
                         out=ga[:],
                         lhsT=wg_dealt[:, a, cols].bitcast(FP8X4),
-                        lhsT_scale=w_scales[0][:, a, cols],
+                        lhsT_scale=w_plane(0, a, t),
                         start=(a == 0),
                         stop=(a == PASSES - 1),
                         **moving(a, h),
                     )
                 nc.scalar.activation(
-                    carry[t][:, h * BANK : (h + 1) * BANK], ga[:], ACT.Sigmoid, bias=neg_bias[:, t : t + 1], scale=-1.0
+                    lean[t][:, h * BANK : (h + 1) * BANK], ga[:], ACT.Tanh, bias=half_bias[:, t : t + 1], scale=0.5
                 )
-
-        made = [keep.tile([P, J], F32, name="made%d" % t) for t in range(PACK)]
-        for t in range(PACK):
-            cols = slice(t * P, (t + 1) * P)
             for h in range(HALVES):
-                ha = psum.tile([P, BANK], F32, name="ha", bufs=3)
-                for a in range(PASSES):
+                ha = psum.tile([P, BANK], F32, name="ha", tag="bank%d" % ((4 * t + 2 + h) % 6))
+                passes = [(wh4_dealt[:, a, cols].bitcast(U8).bitcast(FP4X4), w_plane(1, a, t), a) for a in range(PASSES)]
+                passes += [(whd_codes[a][:, cols].bitcast(FP8X4), whd_scales[a][:, cols], a) for a in range(PASSES)]
+                if t > 0:
+                    passes = passes[::-1]
+                for i, (words, scale_bytes, a) in enumerate(passes):
                     nc.tensor.matmul_mx(
                         out=ha[:],
-                        lhsT=wh4_dealt[:, a, cols].bitcast(U8).bitcast(FP4X4),
-                        lhsT_scale=w_scales[1][:, a, cols],
-                        start=(a == 0),
-                        stop=False,
-                        **moving(a, h),
-                    )
-                for a in range(PASSES):
-                    nc.tensor.matmul_mx(
-                        out=ha[:],
-                        lhsT=whd_codes[:, a, cols].bitcast(FP8X4),
-                        lhsT_scale=whd_scales[:, a, cols],
-                        start=False,
-                        stop=(a == PASSES - 1),
+                        lhsT=words,
+                        lhsT_scale=scale_bytes,
+                        start=(i == 0),
+                        stop=(i == len(passes) - 1),
                         **moving(a, h),
                     )
                 nc.scalar.activation(made[t][:, h * BANK : (h + 1) * BANK], ha[:], ACT.Silu)
 
         y = keep.tile([P, PACK, J], F32, name="y")
         y_rows = out_0.rearrange("(p t) j -> p t j", t=PACK)
+        halves = [slice(h * BANK, (h + 1) * BANK) for h in range(HALVES)]
 
-        def gate_made(t):
-            nc.vector.scalar_tensor_tensor(made[t][:, :], carry[t][:, :], 1.0, made[t][:, :], ALU.subtract, ALU.mult)
+        def entries(js):
+            return offsets[:, js.start // 16 : js.stop // 16]
 
         for t in range(PACK - 1):
-            kept = keep.tile([P, J], F32, name="kept", bufs=2)
-            nc.vector.tensor_tensor(kept[:], r_tiles[t][:].indirect(offsets[:]), carry[t][:, :], ALU.mult)
-            gate_made(t)
-            nc.vector.tensor_tensor(y[:, t, :], kept[:], made[t][:, :], ALU.subtract)
+            gap = keep.tile([P, J], F32, name="gap", bufs=2)
+            for js in halves:
+                nc.vector.tensor_tensor(gap[:, js], r_tiles[t][:].indirect(entries(js)), made[t][:, js], ALU.subtract)
+            for js in halves:
+                nc.vector.scalar_tensor_tensor(gap[:, js], lean[t][:, js], 1.0, gap[:, js], ALU.subtract, ALU.mult)
+            for js in halves:
+                nc.vector.scalar_tensor_tensor(y[:, t, js], gap[:, js], -0.5, made[t][:, js], ALU.mult, ALU.add)
             nc.sync.dma_start(y_rows[:, t, :], y[:, t, :])
         t = PACK - 1
-        gate_made(t)
-        kept = keep.tile([P, J], F32, name="kept", bufs=2)
+        carry = keep.tile([P, J], F32, name="carry")
+        nc.scalar.activation(carry[:], lean[t][:], ACT.Copy, bias=0.5, scale=-0.5)
+        nc.vector.scalar_tensor_tensor(made[t][:], lean[t][:], 1.0, made[t][:], ALU.add, ALU.mult)
+        kept = keep.tile([P, J], F32, name="gap", bufs=2)
 
         y_codes = keep.tile([P, J], I32, name="y_codes", align_bytes=64)
         y_scales = keep.tile([P, J], U8, name="y_scales", align_bytes=64)
@@ -224,14 +199,13 @@ def tile_list_hwayt_dl_siluP_kernel(
         rounded = {}
 
         def look_up(js):
-            nc.vector.tensor_tensor(
-                kept[:, js], r_tiles[t][:].indirect(offsets[:, js.start // 16 : js.stop // 16]), carry[t][:, js], ALU.mult
-            )
+            nc.vector.tensor_tensor(kept[:, js], r_tiles[t][:].indirect(entries(js)), carry[:, js], ALU.mult)
 
         def combine(c, js):
-            nc.vector.tensor_tensor(y[:, t, js], kept[:, js], made[t][:, js], ALU.subtract)
+            nc.vector.scalar_tensor_tensor(y[:, t, js], made[t][:, js], 0.5, kept[:, js], ALU.mult, ALU.add)
             rounded[c] = keep.tile([P, (js.stop - js.start) * PACK], BF16, name="y_round%d" % c, align_bytes=64)
-            nc.scalar.copy(
+            copy = nc.vector.tensor_copy if c == len(chunks) - 1 else nc.scalar.copy
+            copy(
                 rounded[c][:].rearrange("p (c i t) -> p c t i", i=4, t=PACK),
                 y[:, :, js].rearrange("p t (c i) -> p c t i", i=4),
             )

@@ -33,6 +33,7 @@ def tile_list_hwayt_dl_siluP_kernel(
     nc = tc.nc
     with ExitStack() as ctx:
         keep = ctx.enter_context(tc.tile_pool(name="keep", bufs=1))
+        laid = ctx.enter_context(tc.tile_pool(name="laid", bufs=1))
         psum = ctx.enter_context(tc.psum_pool(name="psum", bufs=1))
 
         offsets = keep.tile([P, J // 16], U16, name="offsets")
@@ -61,24 +62,24 @@ def tile_list_hwayt_dl_siluP_kernel(
         nc.sync.dma_start(wh4_raw[:], wh4_words.rearrange("a p c -> p a c").bitcast(I32))
         tab = keep.tile([P, T], I32, name="tab", align_bytes=64)
         nc.sync.dma_start(tab[:], tab_words[0].rearrange("p c i -> p (c i)").bitcast(I32))
+        whd_rows = whd.rearrange("(a p i) n -> a p (i n)", a=PASSES, i=PACK)
+        whd_first = keep.tile([P, PACK * N], F32, name="whd_first", tag="lean01", align_bytes=64)
+        nc.sync.dma_start(whd_first[:], whd_rows[0])
 
-        picked = keep.tile([P, J], U8, name="picked", tag="r2", align_bytes=64)
+        picked = laid.tile([P, J], U8, name="picked", offset=4 * T - J // 2, align_bytes=64)
         nc.vector.tensor_copy(picked[:], tab_rows[:].bitcast(U8).indirect(offsets[:]))
-        staged = keep.tile([P, PLANE // 4], I32, name="staged", tag="r3", align_bytes=64)
+        staged = keep.tile([P, PLANE // 4], I32, name="staged", align_bytes=64)
         nc.vector.tensor_copy(
             staged[:, 0 : 2 * N // 4].bitcast(U8).rearrange("p (w t c i) -> p w c t i", w=2, t=PACK, i=16),
             w_rows[:].bitcast(U8).rearrange("p w (c i t) -> p w c t i", t=PACK, i=16),
         )
         nc.vector.tensor_copy(staged[:, 2 * N // 4 :], picked[:].bitcast(I32))
-        for q in range(4):
+        for q in (0, 2, 1, 3):
             nc.sync.dma_start(planes[32 * q : 32 * q + 4, :], staged[ROWS_AT + 8 * q : ROWS_AT + 8 * q + 8, :])
         plane_bytes = planes[:].bitcast(U8)
-        whd_raw = []
-        for a in range(PASSES):
-            raw = keep.tile([P, PACK * N], F32, name="whd_raw%d" % a, tag="r%d" % (2 + a), align_bytes=64)
-            nc.sync.dma_start(raw[:], whd[a * 512 : (a + 1) * 512, :].rearrange("(p i) n -> p (i n)", i=PACK))
-            whd_raw.append(raw)
-
+        whd_second = laid.tile([P, PACK * N], F32, name="whd_second", offset=4 * T - 4 * PACK * N, align_bytes=64)
+        nc.sync.dma_start(whd_second[:], whd_rows[1])
+        whd_raw = (whd_first, whd_second)
         wg_dealt = keep.tile([P, PASSES, N], I32, name="wg_dealt", align_bytes=64)
         nc.vector.tensor_copy(
             wg_dealt[:].rearrange("p a (t c i) -> p a c t i", t=PACK, i=4),
@@ -94,7 +95,7 @@ def tile_list_hwayt_dl_siluP_kernel(
 
         v_words = []
         for h in range(HALVES):
-            pairs = keep.tile([P, BANK], I32, name="pairs%d" % h, tag="r%d" % h, align_bytes=64)
+            pairs = keep.tile([P, BANK], I32, name="pairs%d" % h, tag="r1", align_bytes=64)
             nc.vector.tensor_copy(
                 pairs[:].bitcast(U32), tab[:].bitcast(U32).indirect(offsets[:, h * 32 : (h + 1) * 32])
             )
@@ -104,8 +105,8 @@ def tile_list_hwayt_dl_siluP_kernel(
 
         whd_grouped, whd_codes, whd_scales = [], [], []
         for a in range(PASSES):
-            grouped = keep.tile([P, N * PACK], BF16, name="whd_grouped%d" % a, align_bytes=64)
-            nc.vector.tensor_copy(
+            grouped = keep.tile([P, N * PACK], BF16, name="whd_grouped%d" % a, tag=("r2", "grouped1")[a], align_bytes=64)
+            (nc.scalar.copy, nc.vector.tensor_copy)[a](
                 grouped[:].rearrange("p (t m i) -> p m t i", t=PACK, i=PACK),
                 whd_raw[a][:].rearrange("p (i m t) -> p m t i", i=PACK, t=PACK),
             )
@@ -120,7 +121,10 @@ def tile_list_hwayt_dl_siluP_kernel(
         r_rows = rT.rearrange("(p t) c -> p t c", t=PACK)
         r_tiles = []
         for t in range(PACK):
-            r_tile = keep.tile([P, T], F32, name="r_tile%d" % t, tag="r%d" % t, align_bytes=64)
+            if t in (0, PACK - 1):
+                r_tile = laid.tile([P, T], F32, name="r_tile%d" % t, offset=4 * T if t == 0 else 0, align_bytes=64)
+            else:
+                r_tile = keep.tile([P, T], F32, name="r_tile%d" % t, tag="r%d" % t, align_bytes=64)
             nc.sync.dma_start(r_tile[:], r_rows[:, t, :])
             r_tiles.append(r_tile)
 
@@ -132,12 +136,15 @@ def tile_list_hwayt_dl_siluP_kernel(
             at = a * PLANE + w * N + t * P
             return plane_bytes[:, at : at + P]
 
-        lean = [keep.tile([P, J], F32, name="lean%d" % t) for t in range(PACK)]
+        lean01 = keep.tile([P, 2, J], F32, name="lean01", tag="lean01", align_bytes=64)
+        lean23 = keep.tile([P, 2, J], F32, name="lean23")
+        lean = [(lean01, lean23)[t // 2][:, t % 2, :] for t in range(PACK)]
         made = [keep.tile([P, J], F32, name="made%d" % t) for t in range(PACK)]
-        for t in range(PACK):
+
+        def gate_sums(t, pair):
             cols = slice(t * P, (t + 1) * P)
             for h in range(HALVES):
-                ga = psum.tile([P, BANK], F32, name="ga", tag="bank%d" % ((4 * t + h) % 6))
+                ga = psum.tile([P, BANK], F32, name="ga", tag="bank%d" % (2 * pair + h))
                 for a in range(PASSES):
                     nc.tensor.matmul_mx(
                         out=ga[:],
@@ -150,8 +157,11 @@ def tile_list_hwayt_dl_siluP_kernel(
                 nc.scalar.activation(
                     lean[t][:, h * BANK : (h + 1) * BANK], ga[:], ACT.Tanh, bias=half_bias[:, t : t + 1], scale=0.5
                 )
+
+        def feature_sums(t, pair):
+            cols = slice(t * P, (t + 1) * P)
             for h in range(HALVES):
-                ha = psum.tile([P, BANK], F32, name="ha", tag="bank%d" % ((4 * t + 2 + h) % 6))
+                ha = psum.tile([P, BANK], F32, name="ha", tag="bank%d" % (2 * pair + h))
                 passes = [(wh4_dealt[:, a, cols].bitcast(U8).bitcast(FP4X4), w_plane(1, a, t), a) for a in range(PASSES)]
                 passes += [(whd_codes[a][:, cols].bitcast(FP8X4), whd_scales[a][:, cols], a) for a in range(PASSES)]
                 if t > 0:
@@ -166,6 +176,10 @@ def tile_list_hwayt_dl_siluP_kernel(
                         **moving(a, h),
                     )
                 nc.scalar.activation(made[t][:, h * BANK : (h + 1) * BANK], ha[:], ACT.Silu)
+
+        for t in range(PACK):
+            gate_sums(t, (2 * t) % 3)
+            feature_sums(t, (2 * t + 1) % 3)
 
         y = keep.tile([P, PACK, J], F32, name="y")
         y_rows = out_0.rearrange("(p t) j -> p t j", t=PACK)
@@ -185,9 +199,8 @@ def tile_list_hwayt_dl_siluP_kernel(
             nc.sync.dma_start(y_rows[:, t, :], y[:, t, :])
         t = PACK - 1
         carry = keep.tile([P, J], F32, name="carry")
-        nc.scalar.activation(carry[:], lean[t][:], ACT.Copy, bias=0.5, scale=-0.5)
-        nc.vector.scalar_tensor_tensor(made[t][:], lean[t][:], 1.0, made[t][:], ALU.add, ALU.mult)
-        kept = keep.tile([P, J], F32, name="gap", bufs=2)
+        nc.scalar.activation(carry[:], lean[t], ACT.Copy, bias=0.5, scale=-0.5)
+        nc.vector.scalar_tensor_tensor(made[t][:], lean[t], 1.0, made[t][:], ALU.add, ALU.mult)
 
         y_codes = keep.tile([P, J], I32, name="y_codes", align_bytes=64)
         y_scales = keep.tile([P, J], U8, name="y_scales", align_bytes=64)
@@ -196,13 +209,14 @@ def tile_list_hwayt_dl_siluP_kernel(
         for width in LAST_CHUNKS:
             j0 = chunks[-1].stop if chunks else 0
             chunks.append(slice(j0, j0 + width))
-        rounded = {}
+        kept, rounded = {}, {}
 
-        def look_up(js):
-            nc.vector.tensor_tensor(kept[:, js], r_tiles[t][:].indirect(entries(js)), carry[:, js], ALU.mult)
+        def look_up(c, js):
+            kept[c] = keep.tile([P, js.stop - js.start], F32, name="kept%d" % c, tag="kept%d" % (c % 2))
+            nc.vector.tensor_tensor(kept[c][:], r_tiles[t][:].indirect(entries(js)), carry[:, js], ALU.mult)
 
         def combine(c, js):
-            nc.vector.scalar_tensor_tensor(y[:, t, js], made[t][:, js], 0.5, kept[:, js], ALU.mult, ALU.add)
+            nc.vector.scalar_tensor_tensor(y[:, t, js], made[t][:, js], 0.5, kept[c][:], ALU.mult, ALU.add)
             rounded[c] = keep.tile([P, (js.stop - js.start) * PACK], BF16, name="y_round%d" % c, align_bytes=64)
             copy = nc.vector.tensor_copy if c == len(chunks) - 1 else nc.scalar.copy
             copy(
@@ -221,7 +235,7 @@ def tile_list_hwayt_dl_siluP_kernel(
 
         for c in range(len(chunks) + 2):
             if c < len(chunks):
-                look_up(chunks[c])
+                look_up(c, chunks[c])
             if c >= 2:
                 quantise(c - 2, chunks[c - 2])
             if 1 <= c <= len(chunks):

@@ -23,8 +23,8 @@ BANK = 512
 HALVES = J // BANK
 ROWS_AT = 96
 PLANE = 2 * N + J
-LAST_CHUNKS = (128, 256, 256, 256, 128)
-STORE_FROM = {384: 0, 896: 384, 1024: 896}
+LAST_CHUNKS = (256, 256, 256, 128, 128)
+STORE_FROM = {512: 0, 896: 512, 1024: 896}
 
 
 def tile_list_hwayt_dl_siluP_kernel(
@@ -56,35 +56,31 @@ def tile_list_hwayt_dl_siluP_kernel(
         nc.gpsimd.memset(warm[:], 0.0)
         nc.scalar.activation(warm_out[:], warm[:], ACT.Silu)
 
-        wg_raw = keep.tile([P, PASSES, N], I32, name="wg_raw", align_bytes=64)
-        nc.sync.dma_start(wg_raw[:], wg_words.rearrange("a p n i -> p a (n i)").bitcast(I32))
         wh4_raw = keep.tile([P, PASSES, N // 2], I32, name="wh4_raw")
         nc.sync.dma_start(wh4_raw[:], wh4_words.rearrange("a p c -> p a c").bitcast(I32))
         tab = keep.tile([P, T], I32, name="tab", align_bytes=64)
         nc.sync.dma_start(tab[:], tab_words[0].rearrange("p c i -> p (c i)").bitcast(I32))
         whd_rows = whd.rearrange("(a p i) n -> a p (i n)", a=PASSES, i=PACK)
-        whd_first = keep.tile([P, PACK * N], F32, name="whd_first", tag="lean01", align_bytes=64)
+        whd_first = laid.tile([P, PACK * N], F32, name="whd_first", offset=9 * T, align_bytes=64)
         nc.sync.dma_start(whd_first[:], whd_rows[0])
 
-        picked = laid.tile([P, J], U8, name="picked", offset=4 * T - J // 2, align_bytes=64)
-        nc.vector.tensor_copy(picked[:], tab_rows[:].bitcast(U8).indirect(offsets[:]))
+        spanning = laid.tile([P, T + J], U8, name="spanning", offset=4 * T - J // 2, align_bytes=64)
+        picked = spanning[:, 0:J]
+        nc.vector.tensor_copy(picked, tab_rows[:].bitcast(U8).indirect(offsets[:]))
         staged = keep.tile([P, PLANE // 4], I32, name="staged", align_bytes=64)
         nc.vector.tensor_copy(
             staged[:, 0 : 2 * N // 4].bitcast(U8).rearrange("p (w t c i) -> p w c t i", w=2, t=PACK, i=16),
             w_rows[:].bitcast(U8).rearrange("p w (c i t) -> p w c t i", t=PACK, i=16),
         )
-        nc.vector.tensor_copy(staged[:, 2 * N // 4 :], picked[:].bitcast(I32))
+        nc.vector.tensor_copy(staged[:, 2 * N // 4 :], picked.bitcast(I32))
         for q in (0, 2, 1, 3):
             nc.sync.dma_start(planes[32 * q : 32 * q + 4, :], staged[ROWS_AT + 8 * q : ROWS_AT + 8 * q + 8, :])
         plane_bytes = planes[:].bitcast(U8)
         whd_second = laid.tile([P, PACK * N], F32, name="whd_second", offset=4 * T - 4 * PACK * N, align_bytes=64)
         nc.sync.dma_start(whd_second[:], whd_rows[1])
         whd_raw = (whd_first, whd_second)
-        wg_dealt = keep.tile([P, PASSES, N], I32, name="wg_dealt", align_bytes=64)
-        nc.vector.tensor_copy(
-            wg_dealt[:].rearrange("p a (t c i) -> p a c t i", t=PACK, i=4),
-            wg_raw[:].rearrange("p a (c i t) -> p a c t i", t=PACK, i=4),
-        )
+        wg_raw = laid.tile([P, PASSES, N], I32, name="wg_raw", offset=4 * T, align_bytes=64)
+        nc.sync.dma_start(wg_raw[:], wg_words.rearrange("a p n i -> p a (n i)").bitcast(I32))
         wh4_dealt = keep.tile([P, PASSES, N], U16, name="wh4_dealt", align_bytes=64)
         nc.vector.tensor_copy(
             wh4_dealt[:].rearrange("p a (t c i) -> p a c t i", t=PACK, i=8),
@@ -95,7 +91,7 @@ def tile_list_hwayt_dl_siluP_kernel(
 
         v_words = []
         for h in range(HALVES):
-            pairs = keep.tile([P, BANK], I32, name="pairs%d" % h, tag="r1", align_bytes=64)
+            pairs = keep.tile([P, BANK], I32, name="pairs%d" % h, tag="r%d" % (1 + h), align_bytes=64)
             nc.vector.tensor_copy(
                 pairs[:].bitcast(U32), tab[:].bitcast(U32).indirect(offsets[:, h * 32 : (h + 1) * 32])
             )
@@ -105,12 +101,17 @@ def tile_list_hwayt_dl_siluP_kernel(
 
         whd_grouped, whd_codes, whd_scales = [], [], []
         for a in range(PASSES):
-            grouped = keep.tile([P, N * PACK], BF16, name="whd_grouped%d" % a, tag=("r2", "grouped1")[a], align_bytes=64)
+            grouped = keep.tile([P, N * PACK], BF16, name="whd_grouped%d" % a, align_bytes=64)
             (nc.scalar.copy, nc.vector.tensor_copy)[a](
                 grouped[:].rearrange("p (t m i) -> p m t i", t=PACK, i=PACK),
                 whd_raw[a][:].rearrange("p (i m t) -> p m t i", i=PACK, t=PACK),
             )
             whd_grouped.append(grouped)
+        wg_dealt = keep.tile([P, PASSES, N], I32, name="wg_dealt", align_bytes=64)
+        nc.vector.tensor_copy(
+            wg_dealt[:].rearrange("p a (t c i) -> p a c t i", t=PACK, i=4),
+            wg_raw[:].rearrange("p a (c i t) -> p a c t i", t=PACK, i=4),
+        )
         for a in range(PASSES):
             codes = keep.tile([P, N], U32, name="whd_codes%d" % a, align_bytes=64)
             scale_bytes = keep.tile([P, N], U8, name="whd_scales%d" % a, align_bytes=64)
@@ -122,7 +123,7 @@ def tile_list_hwayt_dl_siluP_kernel(
         r_tiles = []
         for t in range(PACK):
             if t in (0, PACK - 1):
-                r_tile = laid.tile([P, T], F32, name="r_tile%d" % t, offset=4 * T if t == 0 else 0, align_bytes=64)
+                r_tile = laid.tile([P, T], F32, name="r_tile%d" % t, offset=5 * T if t == 0 else 0, align_bytes=64)
             else:
                 r_tile = keep.tile([P, T], F32, name="r_tile%d" % t, tag="r%d" % t, align_bytes=64)
             nc.sync.dma_start(r_tile[:], r_rows[:, t, :])
@@ -136,9 +137,8 @@ def tile_list_hwayt_dl_siluP_kernel(
             at = a * PLANE + w * N + t * P
             return plane_bytes[:, at : at + P]
 
-        lean01 = keep.tile([P, 2, J], F32, name="lean01", tag="lean01", align_bytes=64)
-        lean23 = keep.tile([P, 2, J], F32, name="lean23")
-        lean = [(lean01, lean23)[t // 2][:, t % 2, :] for t in range(PACK)]
+        lean = [laid.tile([P, J], F32, name="lean%d" % t, offset=9 * T + 4 * J * t, align_bytes=64) for t in range(PACK)]
+        carry = [keep.tile([P, J], F32, name="carry%d" % t) for t in range(PACK)]
         made = [keep.tile([P, J], F32, name="made%d" % t) for t in range(PACK)]
 
         def gate_sums(t, pair):
@@ -157,6 +157,10 @@ def tile_list_hwayt_dl_siluP_kernel(
                 nc.scalar.activation(
                     lean[t][:, h * BANK : (h + 1) * BANK], ga[:], ACT.Tanh, bias=half_bias[:, t : t + 1], scale=0.5
                 )
+            if t == 0:
+                nc.vector.tensor_scalar(carry[t][:], lean[t][:], -0.5, 0.5, ALU.mult, ALU.add)
+            else:
+                nc.scalar.activation(carry[t][:], lean[t][:], ACT.Copy, bias=0.5, scale=-0.5)
 
         def feature_sums(t, pair):
             cols = slice(t * P, (t + 1) * P)
@@ -188,19 +192,20 @@ def tile_list_hwayt_dl_siluP_kernel(
         def entries(js):
             return offsets[:, js.start // 16 : js.stop // 16]
 
+        def gate_made(t):
+            for js in halves if t == 0 else [slice(0, J)]:
+                nc.vector.scalar_tensor_tensor(made[t][:, js], lean[t][:, js], 1.0, made[t][:, js], ALU.add, ALU.mult)
+
         for t in range(PACK - 1):
-            gap = keep.tile([P, J], F32, name="gap", bufs=2)
+            gate_made(t)
+            carried = laid.tile([P, J], F32, name="carried%d" % t, offset=9 * T + 4 * J * t, align_bytes=64)
             for js in halves:
-                nc.vector.tensor_tensor(gap[:, js], r_tiles[t][:].indirect(entries(js)), made[t][:, js], ALU.subtract)
+                nc.vector.tensor_tensor(carried[:, js], r_tiles[t][:].indirect(entries(js)), carry[t][:, js], ALU.mult)
             for js in halves:
-                nc.vector.scalar_tensor_tensor(gap[:, js], lean[t][:, js], 1.0, gap[:, js], ALU.subtract, ALU.mult)
-            for js in halves:
-                nc.vector.scalar_tensor_tensor(y[:, t, js], gap[:, js], -0.5, made[t][:, js], ALU.mult, ALU.add)
+                nc.vector.scalar_tensor_tensor(y[:, t, js], made[t][:, js], 0.5, carried[:, js], ALU.mult, ALU.add)
             nc.sync.dma_start(y_rows[:, t, :], y[:, t, :])
         t = PACK - 1
-        carry = keep.tile([P, J], F32, name="carry")
-        nc.scalar.activation(carry[:], lean[t], ACT.Copy, bias=0.5, scale=-0.5)
-        nc.vector.scalar_tensor_tensor(made[t][:], lean[t], 1.0, made[t][:], ALU.add, ALU.mult)
+        gate_made(t)
 
         y_codes = keep.tile([P, J], I32, name="y_codes", align_bytes=64)
         y_scales = keep.tile([P, J], U8, name="y_scales", align_bytes=64)
@@ -211,18 +216,25 @@ def tile_list_hwayt_dl_siluP_kernel(
             chunks.append(slice(j0, j0 + width))
         kept, rounded = {}, {}
 
+        def round_pair(c, js, u):
+            nc.scalar.copy(
+                rounded[c][:].rearrange("p (j t) -> p j t", t=PACK)[:, :, 2 * u : 2 * u + 2],
+                y[:, 2 * u : 2 * u + 2, js].rearrange("p t j -> p j t"),
+            )
+
+        for c, js in enumerate(chunks):
+            rounded[c] = keep.tile([P, (js.stop - js.start) * PACK], BF16, name="y_round%d" % c, align_bytes=64)
+            round_pair(c, js, 0)
+
         def look_up(c, js):
-            kept[c] = keep.tile([P, js.stop - js.start], F32, name="kept%d" % c, tag="kept%d" % (c % 2))
-            nc.vector.tensor_tensor(kept[c][:], r_tiles[t][:].indirect(entries(js)), carry[:, js], ALU.mult)
+            kept[c] = laid.tile(
+                [P, js.stop - js.start], F32, name="kept%d" % c, offset=9 * T + 4 * J * t + 2 * J * (c % 2), align_bytes=64
+            )
+            nc.vector.tensor_tensor(kept[c][:], r_tiles[t][:].indirect(entries(js)), carry[t][:, js], ALU.mult)
 
         def combine(c, js):
             nc.vector.scalar_tensor_tensor(y[:, t, js], made[t][:, js], 0.5, kept[c][:], ALU.mult, ALU.add)
-            rounded[c] = keep.tile([P, (js.stop - js.start) * PACK], BF16, name="y_round%d" % c, align_bytes=64)
-            copy = nc.vector.tensor_copy if c == len(chunks) - 1 else nc.scalar.copy
-            copy(
-                rounded[c][:].rearrange("p (c i t) -> p c t i", i=4, t=PACK),
-                y[:, :, js].rearrange("p t (c i) -> p c t i", i=4),
-            )
+            round_pair(c, js, 1)
             if js.stop in STORE_FROM:
                 ss = slice(STORE_FROM[js.stop], js.stop)
                 nc.sync.dma_start(y_rows[:, t, ss], y[:, t, ss])

@@ -24,7 +24,7 @@ HALVES = J // BANK
 ROWS_AT = 96
 PLANE = 2 * N + J
 LAST_CHUNKS = (256, 256, 256, 128, 128)
-STORE_FROM = {512: 0, 896: 512, 1024: 896}
+STORE_FROM = {512: 0, 768: 512, 1024: 768}
 
 
 def tile_list_hwayt_dl_siluP_kernel(
@@ -37,11 +37,10 @@ def tile_list_hwayt_dl_siluP_kernel(
         psum = ctx.enter_context(tc.psum_pool(name="psum", bufs=1))
 
         offsets = keep.tile([P, J // 16], U16, name="offsets")
-        nc.sync.dma_start(offsets[:], offs)
-
         tab_rows = keep.tile([P, T // 4], I32, name="tab_rows", align_bytes=64)
         nc.vector.memset(tab_rows[0:ROWS_AT, :], 0)
         nc.sync.dma_start(tab_rows[ROWS_AT:P, :], tab_scales.bitcast(I32).rearrange("a q c -> q a c"))
+        nc.sync.dma_start(offsets[:], offs)
         w_rows = keep.tile([P, 2, N // 4], I32, name="w_rows", align_bytes=64)
         nc.vector.memset(w_rows[0:ROWS_AT, :, :], 0)
         for w, scales in enumerate((wg_scales, wh4_scales)):
@@ -53,13 +52,13 @@ def tile_list_hwayt_dl_siluP_kernel(
         nc.scalar.dma_start(bias[:], bg.rearrange("(p t) -> p t", t=PACK))
         warm = keep.tile([P, 1], F32, name="warm")
         warm_out = keep.tile([P, 1], F32, name="warm_out")
-        nc.gpsimd.memset(warm[:], 0.0)
+        nc.vector.memset(warm[:], 0.0)
         nc.scalar.activation(warm_out[:], warm[:], ACT.Silu)
 
-        wh4_raw = keep.tile([P, PASSES, N // 2], I32, name="wh4_raw")
-        nc.sync.dma_start(wh4_raw[:], wh4_words.rearrange("a p c -> p a c").bitcast(I32))
         tab = keep.tile([P, T], I32, name="tab", align_bytes=64)
         nc.sync.dma_start(tab[:], tab_words[0].rearrange("p c i -> p (c i)").bitcast(I32))
+        wh4_raw = keep.tile([P, PASSES, N // 2], I32, name="wh4_raw")
+        nc.sync.dma_start(wh4_raw[:], wh4_words.rearrange("a p c -> p a c").bitcast(I32))
         whd_rows = whd.rearrange("(a p i) n -> a p (i n)", a=PASSES, i=PACK)
         whd_first = laid.tile([P, PACK * N], F32, name="whd_first", offset=9 * T, align_bytes=64)
         nc.sync.dma_start(whd_first[:], whd_rows[0])
@@ -81,43 +80,52 @@ def tile_list_hwayt_dl_siluP_kernel(
         whd_raw = (whd_first, whd_second)
         wg_raw = laid.tile([P, PASSES, N], I32, name="wg_raw", offset=4 * T, align_bytes=64)
         nc.sync.dma_start(wg_raw[:], wg_words.rearrange("a p n i -> p a (n i)").bitcast(I32))
-        wh4_dealt = keep.tile([P, PASSES, N], U16, name="wh4_dealt", align_bytes=64)
-        nc.vector.tensor_copy(
-            wh4_dealt[:].rearrange("p a (t c i) -> p a c t i", t=PACK, i=8),
-            wh4_raw[:].bitcast(U16).rearrange("p a (c i t) -> p a c t i", t=PACK, i=8),
-        )
         half_bias = keep.tile([P, PACK], F32, name="half_bias")
         nc.vector.tensor_scalar(half_bias[:], bias[:], 0.5, None, ALU.mult)
 
-        v_words = []
+        pairs, v_words = [], []
         for h in range(HALVES):
-            pairs = keep.tile([P, BANK], I32, name="pairs%d" % h, tag="r%d" % (1 + h), align_bytes=64)
+            pairs.append(keep.tile([P, BANK], I32, name="pairs%d" % h, tag="r%d" % (1 + h), align_bytes=64))
             nc.vector.tensor_copy(
-                pairs[:].bitcast(U32), tab[:].bitcast(U32).indirect(offsets[:, h * 32 : (h + 1) * 32])
+                pairs[h][:].bitcast(U32), tab[:].bitcast(U32).indirect(offsets[:, h * 32 : (h + 1) * 32])
             )
+        wh4_dealt = keep.tile([P, PASSES, N], U16, name="wh4_dealt", align_bytes=64)
+        for h in range(HALVES):
             parted = keep.tile([P, PASSES, BANK], U16, name="parted%d" % h, align_bytes=64)
-            nc.vector.tensor_copy(parted[:], pairs[:].bitcast(U16).rearrange("p (j d) -> p d j", d=PASSES))
+            nc.vector.tensor_copy(parted[:], pairs[h][:].bitcast(U16).rearrange("p (j d) -> p d j", d=PASSES))
             v_words.append(parted)
+            if h == 0:
+                nc.vector.tensor_copy(
+                    wh4_dealt[:].rearrange("p a (t c i) -> p a c t i", t=PACK, i=8),
+                    wh4_raw[:].bitcast(U16).rearrange("p a (c i t) -> p a c t i", t=PACK, i=8),
+                )
 
-        whd_grouped, whd_codes, whd_scales = [], [], []
-        for a in range(PASSES):
-            grouped = keep.tile([P, N * PACK], BF16, name="whd_grouped%d" % a, align_bytes=64)
-            (nc.scalar.copy, nc.vector.tensor_copy)[a](
-                grouped[:].rearrange("p (t m i) -> p m t i", t=PACK, i=PACK),
-                whd_raw[a][:].rearrange("p (i m t) -> p m t i", i=PACK, t=PACK),
+        whd_codes = [keep.tile([P, N], U32, name="whd_codes%d" % a, align_bytes=64) for a in range(PASSES)]
+        whd_scales = [keep.tile([P, N], U8, name="whd_scales%d" % a, align_bytes=64) for a in range(PASSES)]
+
+        def round_whd(copy, a, t0, t1):
+            grouped = keep.tile([P, (t1 - t0) * N], BF16, name="whd_grouped%d_%d" % (a, t0), align_bytes=64)
+            copy(
+                grouped[:].rearrange("p (t m i) -> p m t i", t=t1 - t0, i=PACK),
+                whd_raw[a][:].rearrange("p (i m t) -> p m t i", i=PACK, t=PACK)[:, :, t0:t1, :],
             )
-            whd_grouped.append(grouped)
+            return grouped
+
+        def quantise_whd(grouped, a, t0, t1):
+            cols = slice(t0 * P, t1 * P)
+            nc.vector.quantize_mx(out=whd_codes[a][:, cols].bitcast(FP8X4), scales=whd_scales[a][:, cols], in_=grouped[:])
+
+        first = round_whd(nc.scalar.copy, 0, 0, PACK)
+        second_low = round_whd(nc.vector.tensor_copy, 1, 0, 2)
+        second_high = round_whd(nc.scalar.copy, 1, 2, PACK)
+        quantise_whd(first, 0, 0, PACK)
+        quantise_whd(second_low, 1, 0, 2)
         wg_dealt = keep.tile([P, PASSES, N], I32, name="wg_dealt", align_bytes=64)
         nc.vector.tensor_copy(
             wg_dealt[:].rearrange("p a (t c i) -> p a c t i", t=PACK, i=4),
             wg_raw[:].rearrange("p a (c i t) -> p a c t i", t=PACK, i=4),
         )
-        for a in range(PASSES):
-            codes = keep.tile([P, N], U32, name="whd_codes%d" % a, align_bytes=64)
-            scale_bytes = keep.tile([P, N], U8, name="whd_scales%d" % a, align_bytes=64)
-            nc.vector.quantize_mx(out=codes[:].bitcast(FP8X4), scales=scale_bytes[:], in_=whd_grouped[a][:])
-            whd_codes.append(codes)
-            whd_scales.append(scale_bytes)
+        quantise_whd(second_high, 1, 2, PACK)
 
         r_rows = rT.rearrange("(p t) c -> p t c", t=PACK)
         r_tiles = []
@@ -138,7 +146,13 @@ def tile_list_hwayt_dl_siluP_kernel(
             return plane_bytes[:, at : at + P]
 
         lean = [laid.tile([P, J], F32, name="lean%d" % t, offset=9 * T + 4 * J * t, align_bytes=64) for t in range(PACK)]
-        carry = [keep.tile([P, J], F32, name="carry%d" % t) for t in range(PACK)]
+        carry = [
+            [
+                laid.tile([P, BANK], F32, name="carry%d_0" % t, offset=13 * T + 4 * J * t, align_bytes=64),
+                keep.tile([P, BANK], F32, name="carry%d_1" % t),
+            ]
+            for t in range(PACK)
+        ]
         made = [keep.tile([P, J], F32, name="made%d" % t) for t in range(PACK)]
 
         def gate_sums(t, pair):
@@ -157,10 +171,8 @@ def tile_list_hwayt_dl_siluP_kernel(
                 nc.scalar.activation(
                     lean[t][:, h * BANK : (h + 1) * BANK], ga[:], ACT.Tanh, bias=half_bias[:, t : t + 1], scale=0.5
                 )
-            if t == 0:
-                nc.vector.tensor_scalar(carry[t][:], lean[t][:], -0.5, 0.5, ALU.mult, ALU.add)
-            else:
-                nc.scalar.activation(carry[t][:], lean[t][:], ACT.Copy, bias=0.5, scale=-0.5)
+            for h in range(HALVES):
+                nc.scalar.activation(carry[t][h][:], lean[t][:, h * BANK : (h + 1) * BANK], ACT.Copy, bias=0.5, scale=-0.5)
 
         def feature_sums(t, pair):
             cols = slice(t * P, (t + 1) * P)
@@ -182,8 +194,8 @@ def tile_list_hwayt_dl_siluP_kernel(
                 nc.scalar.activation(made[t][:, h * BANK : (h + 1) * BANK], ha[:], ACT.Silu)
 
         for t in range(PACK):
-            gate_sums(t, (2 * t) % 3)
-            feature_sums(t, (2 * t + 1) % 3)
+            feature_sums(t, (2 * t) % 4)
+            gate_sums(t, (2 * t + 1) % 4)
 
         y = keep.tile([P, PACK, J], F32, name="y")
         y_rows = out_0.rearrange("(p t) j -> p t j", t=PACK)
@@ -192,20 +204,25 @@ def tile_list_hwayt_dl_siluP_kernel(
         def entries(js):
             return offsets[:, js.start // 16 : js.stop // 16]
 
-        def gate_made(t):
-            for js in halves if t == 0 else [slice(0, J)]:
-                nc.vector.scalar_tensor_tensor(made[t][:, js], lean[t][:, js], 1.0, made[t][:, js], ALU.add, ALU.mult)
+        gated = {}
 
+        def gate_made(t):
+            if t == 0:
+                gated[t] = keep.tile([P, J], F32, name="gated0")
+            else:
+                gated[t] = laid.tile([P, J], F32, name="gated%d" % t, offset=13 * T + 4 * J * (t - 1), align_bytes=64)
+            for js in halves if t == 0 else [slice(0, J)]:
+                nc.vector.scalar_tensor_tensor(gated[t][:, js], lean[t][:, js], 1.0, made[t][:, js], ALU.add, ALU.mult)
+
+        gate_made(0)
         for t in range(PACK - 1):
-            gate_made(t)
-            carried = laid.tile([P, J], F32, name="carried%d" % t, offset=9 * T + 4 * J * t, align_bytes=64)
-            for js in halves:
-                nc.vector.tensor_tensor(carried[:, js], r_tiles[t][:].indirect(entries(js)), carry[t][:, js], ALU.mult)
-            for js in halves:
-                nc.vector.scalar_tensor_tensor(y[:, t, js], made[t][:, js], 0.5, carried[:, js], ALU.mult, ALU.add)
+            carried = keep.tile([P, J], F32, name="carried%d" % t, tag="carried%d" % (t % 2))
+            for h, js in enumerate(halves):
+                nc.vector.tensor_tensor(carried[:, js], r_tiles[t][:].indirect(entries(js)), carry[t][h][:], ALU.mult)
+            gate_made(t + 1)
+            nc.vector.scalar_tensor_tensor(y[:, t, :], gated[t][:], 0.5, carried[:], ALU.mult, ALU.add)
             nc.sync.dma_start(y_rows[:, t, :], y[:, t, :])
         t = PACK - 1
-        gate_made(t)
 
         y_codes = keep.tile([P, J], I32, name="y_codes", align_bytes=64)
         y_scales = keep.tile([P, J], U8, name="y_scales", align_bytes=64)
@@ -228,12 +245,14 @@ def tile_list_hwayt_dl_siluP_kernel(
 
         def look_up(c, js):
             kept[c] = laid.tile(
-                [P, js.stop - js.start], F32, name="kept%d" % c, offset=9 * T + 4 * J * t + 2 * J * (c % 2), align_bytes=64
+                [P, js.stop - js.start], F32, name="kept%d" % c, offset=9 * T + J * (c % 3), align_bytes=64
             )
-            nc.vector.tensor_tensor(kept[c][:], r_tiles[t][:].indirect(entries(js)), carry[t][:, js], ALU.mult)
+            at = js.start % BANK
+            share = carry[t][js.start // BANK][:, at : at + js.stop - js.start]
+            nc.vector.tensor_tensor(kept[c][:], r_tiles[t][:].indirect(entries(js)), share, ALU.mult)
 
         def combine(c, js):
-            nc.vector.scalar_tensor_tensor(y[:, t, js], made[t][:, js], 0.5, kept[c][:], ALU.mult, ALU.add)
+            nc.vector.scalar_tensor_tensor(y[:, t, js], gated[t][:, js], 0.5, kept[c][:], ALU.mult, ALU.add)
             round_pair(c, js, 1)
             if js.stop in STORE_FROM:
                 ss = slice(STORE_FROM[js.stop], js.stop)

@@ -100,32 +100,37 @@ def tile_list_hwayt_dl_siluP_kernel(
                     wh4_raw[:].bitcast(U16).rearrange("p a (c i t) -> p a c t i", t=PACK, i=8),
                 )
 
-        whd_codes = [keep.tile([P, N], U32, name="whd_codes%d" % a, align_bytes=64) for a in range(PASSES)]
-        whd_scales = [keep.tile([P, N], U8, name="whd_scales%d" % a, align_bytes=64) for a in range(PASSES)]
+        whd_codes = keep.tile([P, 2, PASSES, N // 2], U32, name="whd_codes", align_bytes=64)
+        whd_scales = keep.tile([P, 2, PASSES, N // 2], U8, name="whd_scales", align_bytes=64)
+        whd_grouped = [
+            keep.tile([P, PASSES * 2 * N], BF16, name="whd_grouped%d" % u, align_bytes=64) for u in range(2)
+        ]
 
-        def round_whd(copy, a, t0, t1):
-            grouped = keep.tile([P, (t1 - t0) * N], BF16, name="whd_grouped%d_%d" % (a, t0), align_bytes=64)
+        def round_whd(copy, a, u):
             copy(
-                grouped[:].rearrange("p (t m i) -> p m t i", t=t1 - t0, i=PACK),
-                whd_raw[a][:].rearrange("p (i m t) -> p m t i", i=PACK, t=PACK)[:, :, t0:t1, :],
+                whd_grouped[u][:, a * 2 * N : (a + 1) * 2 * N].rearrange("p (t m i) -> p m t i", t=2, i=PACK),
+                whd_raw[a][:].rearrange("p (i m t) -> p m t i", i=PACK, t=PACK)[:, :, 2 * u : 2 * u + 2, :],
             )
-            return grouped
 
-        def quantise_whd(grouped, a, t0, t1):
-            cols = slice(t0 * P, t1 * P)
-            nc.vector.quantize_mx(out=whd_codes[a][:, cols].bitcast(FP8X4), scales=whd_scales[a][:, cols], in_=grouped[:])
+        def quantise_whd(u, a0, a1):
+            nc.vector.quantize_mx(
+                out=whd_codes[:, u, a0:a1, :].rearrange("p a n -> p (a n)").bitcast(FP8X4),
+                scales=whd_scales[:, u, a0:a1, :].rearrange("p a n -> p (a n)"),
+                in_=whd_grouped[u][:, a0 * 2 * N : a1 * 2 * N],
+            )
 
-        first = round_whd(nc.scalar.copy, 0, 0, PACK)
-        second_low = round_whd(nc.vector.tensor_copy, 1, 0, 2)
-        second_high = round_whd(nc.scalar.copy, 1, 2, PACK)
-        quantise_whd(first, 0, 0, PACK)
-        quantise_whd(second_low, 1, 0, 2)
+        round_whd(nc.scalar.copy, 0, 0)
+        quantise_whd(0, 0, 1)
+        round_whd(nc.vector.tensor_copy, 1, 0)
+        quantise_whd(0, 1, 2)
+        for a in range(PASSES):
+            round_whd(nc.scalar.copy, a, 1)
         wg_dealt = keep.tile([P, PASSES, N], I32, name="wg_dealt", align_bytes=64)
         nc.vector.tensor_copy(
             wg_dealt[:].rearrange("p a (t c i) -> p a c t i", t=PACK, i=4),
             wg_raw[:].rearrange("p a (c i t) -> p a c t i", t=PACK, i=4),
         )
-        quantise_whd(second_high, 1, 2, PACK)
+        quantise_whd(1, 0, PASSES)
 
         r_rows = rT.rearrange("(p t) c -> p t c", t=PACK)
         r_tiles = []
@@ -148,89 +153,103 @@ def tile_list_hwayt_dl_siluP_kernel(
         lean = [laid.tile([P, J], F32, name="lean%d" % t, offset=9 * T + 4 * J * t, align_bytes=64) for t in range(PACK)]
         carry = [
             [
-                laid.tile([P, BANK], F32, name="carry%d_0" % t, offset=13 * T + 4 * J * t, align_bytes=64),
-                keep.tile([P, BANK], F32, name="carry%d_1" % t),
+                laid.tile([P, BANK], F32, name="carry%d_%d" % (t, h), offset=13 * T + 4 * J * t + 2 * J * h, align_bytes=64)
+                for h in range(HALVES)
             ]
-            for t in range(PACK)
+            for t in range(PACK - 1)
+        ]
+        chunks = []
+        for width in LAST_CHUNKS:
+            j0 = chunks[-1].stop if chunks else 0
+            chunks.append(slice(j0, j0 + width))
+        last_carry = [
+            laid.tile([P, js.stop - js.start], F32, name="last_carry%d" % c, offset=16 * T + J * c, align_bytes=64)
+            for c, js in enumerate(chunks)
         ]
         made = [keep.tile([P, J], F32, name="made%d" % t) for t in range(PACK)]
 
-        def gate_sums(t, pair):
-            cols = slice(t * P, (t + 1) * P)
-            for h in range(HALVES):
-                ga = psum.tile([P, BANK], F32, name="ga", tag="bank%d" % (2 * pair + h))
-                for a in range(PASSES):
-                    nc.tensor.matmul_mx(
-                        out=ga[:],
-                        lhsT=wg_dealt[:, a, cols].bitcast(FP8X4),
-                        lhsT_scale=w_plane(0, a, t),
-                        start=(a == 0),
-                        stop=(a == PASSES - 1),
-                        **moving(a, h),
-                    )
-                nc.scalar.activation(
-                    lean[t][:, h * BANK : (h + 1) * BANK], ga[:], ACT.Tanh, bias=half_bias[:, t : t + 1], scale=0.5
-                )
-            for h in range(HALVES):
-                nc.scalar.activation(carry[t][h][:], lean[t][:, h * BANK : (h + 1) * BANK], ACT.Copy, bias=0.5, scale=-0.5)
+        halves = [slice(h * BANK, (h + 1) * BANK) for h in range(HALVES)]
 
-        def feature_sums(t, pair):
+        def gate_sum(t, h):
             cols = slice(t * P, (t + 1) * P)
-            for h in range(HALVES):
-                ha = psum.tile([P, BANK], F32, name="ha", tag="bank%d" % (2 * pair + h))
-                passes = [(wh4_dealt[:, a, cols].bitcast(U8).bitcast(FP4X4), w_plane(1, a, t), a) for a in range(PASSES)]
-                passes += [(whd_codes[a][:, cols].bitcast(FP8X4), whd_scales[a][:, cols], a) for a in range(PASSES)]
-                if t > 0:
-                    passes = passes[::-1]
-                for i, (words, scale_bytes, a) in enumerate(passes):
-                    nc.tensor.matmul_mx(
-                        out=ha[:],
-                        lhsT=words,
-                        lhsT_scale=scale_bytes,
-                        start=(i == 0),
-                        stop=(i == len(passes) - 1),
-                        **moving(a, h),
-                    )
-                nc.scalar.activation(made[t][:, h * BANK : (h + 1) * BANK], ha[:], ACT.Silu)
+            ga = psum.tile([P, BANK], F32, name="ga", tag="bank%d" % (4 * (t % 2) + 2 + h))
+            for a in range(PASSES):
+                nc.tensor.matmul_mx(
+                    out=ga[:],
+                    lhsT=wg_dealt[:, a, cols].bitcast(FP8X4),
+                    lhsT_scale=w_plane(0, a, t),
+                    start=(a == 0),
+                    stop=(a == PASSES - 1),
+                    **moving(a, h),
+                )
+            nc.scalar.activation(lean[t][:, halves[h]], ga[:], ACT.Tanh, bias=half_bias[:, t : t + 1], scale=0.5)
+
+        def feature_sum(t, h):
+            cols = slice(t * P, (t + 1) * P)
+            ha = psum.tile([P, BANK], F32, name="ha", tag="bank%d" % (4 * (t % 2) + h))
+            passes = [(wh4_dealt[:, a, cols].bitcast(U8).bitcast(FP4X4), w_plane(1, a, t), a) for a in range(PASSES)]
+            part = slice((t % 2) * P, (t % 2 + 1) * P)
+            passes += [
+                (whd_codes[:, t // 2, a, part].bitcast(FP8X4), whd_scales[:, t // 2, a, part], a) for a in range(PASSES)
+            ]
+            if t > 0:
+                passes = passes[::-1]
+            for i, (words, scale_bytes, a) in enumerate(passes):
+                nc.tensor.matmul_mx(
+                    out=ha[:],
+                    lhsT=words,
+                    lhsT_scale=scale_bytes,
+                    start=(i == 0),
+                    stop=(i == len(passes) - 1),
+                    **moving(a, h),
+                )
+            nc.scalar.activation(made[t][:, halves[h]], ha[:], ACT.Silu)
 
         for t in range(PACK):
-            feature_sums(t, (2 * t) % 4)
-            gate_sums(t, (2 * t + 1) % 4)
+            if t == 0:
+                for one_sum in (feature_sum, gate_sum):
+                    for h in range(HALVES):
+                        one_sum(t, h)
+            else:
+                for h in range(HALVES):
+                    feature_sum(t, h)
+                    gate_sum(t, h)
+            shares = zip(carry[t], halves) if t < PACK - 1 else zip(last_carry, chunks)
+            for share, js in shares:
+                nc.scalar.activation(share[:], lean[t][:, js], ACT.Copy, bias=0.5, scale=-0.5)
 
         y = keep.tile([P, PACK, J], F32, name="y")
         y_rows = out_0.rearrange("(p t) j -> p t j", t=PACK)
-        halves = [slice(h * BANK, (h + 1) * BANK) for h in range(HALVES)]
 
         def entries(js):
             return offsets[:, js.start // 16 : js.stop // 16]
 
         gated = {}
 
-        def gate_made(t):
+        def gate_made(t, h):
             if t == 0:
-                gated[t] = keep.tile([P, J], F32, name="gated0")
+                gated[t, h] = keep.tile([P, BANK], F32, name="gated0_%d" % h)
             else:
-                gated[t] = laid.tile([P, J], F32, name="gated%d" % t, offset=13 * T + 4 * J * (t - 1), align_bytes=64)
-            for js in halves if t == 0 else [slice(0, J)]:
-                nc.vector.scalar_tensor_tensor(gated[t][:, js], lean[t][:, js], 1.0, made[t][:, js], ALU.add, ALU.mult)
+                at = 13 * T + 4 * J * (t - 1) + 2 * J * h
+                gated[t, h] = laid.tile([P, BANK], F32, name="gated%d_%d" % (t, h), offset=at, align_bytes=64)
+            js = halves[h]
+            nc.vector.scalar_tensor_tensor(gated[t, h][:], lean[t][:, js], 1.0, made[t][:, js], ALU.add, ALU.mult)
 
-        gate_made(0)
+        for h in range(HALVES):
+            gate_made(0, h)
         for t in range(PACK - 1):
             carried = keep.tile([P, J], F32, name="carried%d" % t, tag="carried%d" % (t % 2))
             for h, js in enumerate(halves):
                 nc.vector.tensor_tensor(carried[:, js], r_tiles[t][:].indirect(entries(js)), carry[t][h][:], ALU.mult)
-            gate_made(t + 1)
-            nc.vector.scalar_tensor_tensor(y[:, t, :], gated[t][:], 0.5, carried[:], ALU.mult, ALU.add)
+            for h, js in enumerate(halves):
+                nc.vector.scalar_tensor_tensor(y[:, t, js], gated[t, h][:], 0.5, carried[:, js], ALU.mult, ALU.add)
+                gate_made(t + 1, h)
             nc.sync.dma_start(y_rows[:, t, :], y[:, t, :])
         t = PACK - 1
 
         y_codes = keep.tile([P, J], I32, name="y_codes", align_bytes=64)
         y_scales = keep.tile([P, J], U8, name="y_scales", align_bytes=64)
         code_rows = out_1[0].rearrange("p j i -> p (j i)").bitcast(I32)
-        chunks = []
-        for width in LAST_CHUNKS:
-            j0 = chunks[-1].stop if chunks else 0
-            chunks.append(slice(j0, j0 + width))
         kept, rounded = {}, {}
 
         def round_pair(c, js, u):
@@ -245,14 +264,14 @@ def tile_list_hwayt_dl_siluP_kernel(
 
         def look_up(c, js):
             kept[c] = laid.tile(
-                [P, js.stop - js.start], F32, name="kept%d" % c, offset=9 * T + J * (c % 3), align_bytes=64
+                [P, js.stop - js.start], F32, name="kept%d" % c, offset=(9 * T + J * c if c < 2 else 16 * T + J * (c - 2)), align_bytes=64
             )
-            at = js.start % BANK
-            share = carry[t][js.start // BANK][:, at : at + js.stop - js.start]
-            nc.vector.tensor_tensor(kept[c][:], r_tiles[t][:].indirect(entries(js)), share, ALU.mult)
+            nc.vector.tensor_tensor(kept[c][:], r_tiles[t][:].indirect(entries(js)), last_carry[c][:], ALU.mult)
 
         def combine(c, js):
-            nc.vector.scalar_tensor_tensor(y[:, t, js], gated[t][:, js], 0.5, kept[c][:], ALU.mult, ALU.add)
+            at = js.start % BANK
+            share = gated[t, js.start // BANK][:, at : at + js.stop - js.start]
+            nc.vector.scalar_tensor_tensor(y[:, t, js], share, 0.5, kept[c][:], ALU.mult, ALU.add)
             round_pair(c, js, 1)
             if js.stop in STORE_FROM:
                 ss = slice(STORE_FROM[js.stop], js.stop)
@@ -264,13 +283,13 @@ def tile_list_hwayt_dl_siluP_kernel(
                 ss = slice(STORE_FROM[js.stop], js.stop)
                 nc.sync.dma_start(code_rows[:, ss], y_codes[:, ss])
 
-        for c in range(len(chunks) + 2):
+        for c in range(len(chunks) + 1):
             if c < len(chunks):
                 look_up(c, chunks[c])
-            if c >= 2:
-                quantise(c - 2, chunks[c - 2])
-            if 1 <= c <= len(chunks):
+            if c >= 1:
                 combine(c - 1, chunks[c - 1])
+        for c, js in enumerate(chunks):
+            quantise(c, js)
         for q in range(4):
             queue = nc.scalar if q % 2 else nc.sync
             queue.dma_start(

@@ -23,7 +23,8 @@ BANK = 512
 HALVES = J // BANK
 ROWS_AT = 96
 PLANE = 2 * N + J
-LAST_CHUNKS = (256, 256, 256, 128, 128)
+LAST_CHUNKS = (128,) * 8
+CODE_CHUNKS = (256, 256, 256, 128, 128)
 STORE_FROM = {512: 0, 768: 512, 1024: 768}
 
 
@@ -72,8 +73,8 @@ def tile_list_hwayt_dl_siluP_kernel(
             w_rows[:].bitcast(U8).rearrange("p w (c i t) -> p w c t i", t=PACK, i=16),
         )
         nc.vector.tensor_copy(staged[:, 2 * N // 4 :], picked.bitcast(I32))
-        for q in (0, 2, 1, 3):
-            nc.sync.dma_start(planes[32 * q : 32 * q + 4, :], staged[ROWS_AT + 8 * q : ROWS_AT + 8 * q + 8, :])
+        for q in range(4):
+            (nc.sync, nc.scalar)[q // 2].dma_start(planes[32 * q : 32 * q + 4, :], staged[ROWS_AT + 8 * q : ROWS_AT + 8 * q + 8, :])
         plane_bytes = planes[:].bitcast(U8)
         whd_second = laid.tile([P, PACK * N], F32, name="whd_second", offset=4 * T - 4 * PACK * N, align_bytes=64)
         nc.sync.dma_start(whd_second[:], whd_rows[1])
@@ -163,7 +164,7 @@ def tile_list_hwayt_dl_siluP_kernel(
             j0 = chunks[-1].stop if chunks else 0
             chunks.append(slice(j0, j0 + width))
         last_carry = [
-            laid.tile([P, js.stop - js.start], F32, name="last_carry%d" % c, offset=16 * T + J * c, align_bytes=64)
+            laid.tile([P, js.stop - js.start], F32, name="last_carry%d" % c, offset=16 * T + BANK * c, align_bytes=64)
             for c, js in enumerate(chunks)
         ]
         made = [keep.tile([P, J], F32, name="made%d" % t) for t in range(PACK)]
@@ -250,21 +251,21 @@ def tile_list_hwayt_dl_siluP_kernel(
         y_codes = keep.tile([P, J], I32, name="y_codes", align_bytes=64)
         y_scales = keep.tile([P, J], U8, name="y_scales", align_bytes=64)
         code_rows = out_1[0].rearrange("p j i -> p (j i)").bitcast(I32)
-        kept, rounded = {}, {}
+        kept = {}
+        rounded = keep.tile([P, J * PACK], BF16, name="rounded", align_bytes=64)
 
         def round_pair(c, js, u):
             nc.scalar.copy(
-                rounded[c][:].rearrange("p (j t) -> p j t", t=PACK)[:, :, 2 * u : 2 * u + 2],
+                rounded[:].rearrange("p (j t) -> p j t", t=PACK)[:, js, 2 * u : 2 * u + 2],
                 y[:, 2 * u : 2 * u + 2, js].rearrange("p t j -> p j t"),
             )
 
-        for c, js in enumerate(chunks):
-            rounded[c] = keep.tile([P, (js.stop - js.start) * PACK], BF16, name="y_round%d" % c, align_bytes=64)
+        for c, js in enumerate(halves):
             round_pair(c, js, 0)
 
         def look_up(c, js):
             kept[c] = laid.tile(
-                [P, js.stop - js.start], F32, name="kept%d" % c, offset=(9 * T + J * c if c < 2 else 16 * T + J * (c - 2)), align_bytes=64
+                [P, js.stop - js.start], F32, name="kept%d" % c, offset=(9 * T + J * c if c < 2 else 16 * T + BANK * (c - 2)), align_bytes=64
             )
             nc.vector.tensor_tensor(kept[c][:], r_tiles[t][:].indirect(entries(js)), last_carry[c][:], ALU.mult)
 
@@ -278,7 +279,7 @@ def tile_list_hwayt_dl_siluP_kernel(
                 nc.sync.dma_start(y_rows[:, t, ss], y[:, t, ss])
 
         def quantise(c, js):
-            nc.vector.quantize_mx(out=y_codes[:, js].bitcast(FP8X4), scales=y_scales[:, js], in_=rounded[c][:])
+            nc.vector.quantize_mx(out=y_codes[:, js].bitcast(FP8X4), scales=y_scales[:, js], in_=rounded[:, PACK * js.start : PACK * js.stop])
             if js.stop in STORE_FROM:
                 ss = slice(STORE_FROM[js.stop], js.stop)
                 nc.sync.dma_start(code_rows[:, ss], y_codes[:, ss])
@@ -288,8 +289,10 @@ def tile_list_hwayt_dl_siluP_kernel(
                 look_up(c, chunks[c])
             if c >= 1:
                 combine(c - 1, chunks[c - 1])
-        for c, js in enumerate(chunks):
-            quantise(c, js)
+        j0 = 0
+        for c, width in enumerate(CODE_CHUNKS):
+            quantise(c, slice(j0, j0 + width))
+            j0 = j0 + width
         for q in range(4):
             queue = nc.scalar if q % 2 else nc.sync
             queue.dma_start(

@@ -76,11 +76,11 @@ def tile_list_hwayt_dl_siluP_kernel(
         for q in range(4):
             (nc.sync, nc.scalar)[q // 2].dma_start(planes[32 * q : 32 * q + 4, :], staged[ROWS_AT + 8 * q : ROWS_AT + 8 * q + 8, :])
         plane_bytes = planes[:].bitcast(U8)
+        wg_raw = laid.tile([P, PASSES, N], I32, name="wg_raw", offset=4 * T, align_bytes=64)
+        nc.sync.dma_start(wg_raw[:], wg_words.rearrange("a p n i -> p a (n i)").bitcast(I32))
         whd_second = laid.tile([P, PACK * N], F32, name="whd_second", offset=4 * T - 4 * PACK * N, align_bytes=64)
         nc.sync.dma_start(whd_second[:], whd_rows[1])
         whd_raw = (whd_first, whd_second)
-        wg_raw = laid.tile([P, PASSES, N], I32, name="wg_raw", offset=4 * T, align_bytes=64)
-        nc.sync.dma_start(wg_raw[:], wg_words.rearrange("a p n i -> p a (n i)").bitcast(I32))
         half_bias = keep.tile([P, PACK], F32, name="half_bias")
         nc.vector.tensor_scalar(half_bias[:], bias[:], 0.5, None, ALU.mult)
 
@@ -91,47 +91,51 @@ def tile_list_hwayt_dl_siluP_kernel(
                 pairs[h][:].bitcast(U32), tab[:].bitcast(U32).indirect(offsets[:, h * 32 : (h + 1) * 32])
             )
         wh4_dealt = keep.tile([P, PASSES, N], U16, name="wh4_dealt", align_bytes=64)
+        for a in range(PASSES):
+            nc.scalar.copy(
+                wh4_dealt[:, a, :].rearrange("p (t m) -> p m t", t=PACK),
+                wh4_raw[:, a, :].bitcast(U16).rearrange("p (m t) -> p m t", t=PACK),
+            )
         for h in range(HALVES):
             parted = keep.tile([P, PASSES, BANK], U16, name="parted%d" % h, align_bytes=64)
             nc.vector.tensor_copy(parted[:], pairs[h][:].bitcast(U16).rearrange("p (j d) -> p d j", d=PASSES))
             v_words.append(parted)
-            if h == 0:
-                nc.vector.tensor_copy(
-                    wh4_dealt[:].rearrange("p a (t c i) -> p a c t i", t=PACK, i=8),
-                    wh4_raw[:].bitcast(U16).rearrange("p a (c i t) -> p a c t i", t=PACK, i=8),
-                )
 
-        whd_codes = keep.tile([P, 2, PASSES, N // 2], U32, name="whd_codes", align_bytes=64)
+        whd_codes = [keep.tile([P, PASSES, N // 2], U32, name="whd_codes0", align_bytes=64)]
         whd_scales = keep.tile([P, 2, PASSES, N // 2], U8, name="whd_scales", align_bytes=64)
-        whd_grouped = [
-            keep.tile([P, PASSES * 2 * N], BF16, name="whd_grouped%d" % u, align_bytes=64) for u in range(2)
-        ]
+        whd_grouped = {
+            (a, u): keep.tile([P, 2 * N], BF16, name="whd_grouped%d_%d" % (a, u), align_bytes=64)
+            for a, u in ((0, 0), (0, 1))
+        }
 
         def round_whd(copy, a, u):
             copy(
-                whd_grouped[u][:, a * 2 * N : (a + 1) * 2 * N].rearrange("p (t m i) -> p m t i", t=2, i=PACK),
-                whd_raw[a][:].rearrange("p (i m t) -> p m t i", i=PACK, t=PACK)[:, :, 2 * u : 2 * u + 2, :],
+                whd_grouped[a, u][:].rearrange("p (t m i) -> p m i t", t=2, i=PACK),
+                whd_raw[a][:].rearrange("p (i m t) -> p m i t", i=PACK, t=PACK)[:, :, :, 2 * u : 2 * u + 2],
             )
 
-        def quantise_whd(u, a0, a1):
+        def quantise_whd(a, u):
             nc.vector.quantize_mx(
-                out=whd_codes[:, u, a0:a1, :].rearrange("p a n -> p (a n)").bitcast(FP8X4),
-                scales=whd_scales[:, u, a0:a1, :].rearrange("p a n -> p (a n)"),
-                in_=whd_grouped[u][:, a0 * 2 * N : a1 * 2 * N],
+                out=whd_codes[u][:, a, :].bitcast(FP8X4), scales=whd_scales[:, u, a, :], in_=whd_grouped[a, u][:]
             )
 
         round_whd(nc.scalar.copy, 0, 0)
-        quantise_whd(0, 0, 1)
-        round_whd(nc.vector.tensor_copy, 1, 0)
-        quantise_whd(0, 1, 2)
-        for a in range(PASSES):
-            round_whd(nc.scalar.copy, a, 1)
-        wg_dealt = keep.tile([P, PASSES, N], I32, name="wg_dealt", align_bytes=64)
-        nc.vector.tensor_copy(
-            wg_dealt[:].rearrange("p a (t c i) -> p a c t i", t=PACK, i=4),
-            wg_raw[:].rearrange("p a (c i t) -> p a c t i", t=PACK, i=4),
-        )
-        quantise_whd(1, 0, PASSES)
+        quantise_whd(0, 0)
+        round_whd(nc.scalar.copy, 0, 1)
+        wg_dealt = [keep.tile([P, PASSES, N // 2], I32, name="wg_dealt%d" % u, align_bytes=64) for u in range(2)]
+        for u in range(2):
+            nc.vector.tensor_copy(
+                wg_dealt[u][:].rearrange("p a (t m) -> p a m t", t=2),
+                wg_raw[:].rearrange("p a (m t) -> p a m t", t=PACK)[:, :, :, 2 * u : 2 * u + 2],
+            )
+        whd_codes.append(laid.tile([P, PASSES, N // 2], U32, name="whd_codes1", offset=4 * T, align_bytes=64))
+        quantise_whd(0, 1)
+        for u in range(2):
+            whd_grouped[1, u] = laid.tile(
+                [P, 2 * N], BF16, name="whd_grouped1_%d" % u, offset=13 * T + J + 3 * BANK * u, align_bytes=64
+            )
+            round_whd(nc.vector.tensor_copy, 1, u)
+            quantise_whd(1, u)
 
         r_rows = rT.rearrange("(p t) c -> p t c", t=PACK)
         r_tiles = []
@@ -171,13 +175,17 @@ def tile_list_hwayt_dl_siluP_kernel(
 
         halves = [slice(h * BANK, (h + 1) * BANK) for h in range(HALVES)]
 
+        feature_bank = (0, 1, 4, 5, 2, 3, 6, 7)
+        gate_bank = (2, 3, 6, 0, 1, 4, 5, 2)
+        EARLY = 3
+
         def gate_sum(t, h):
-            cols = slice(t * P, (t + 1) * P)
-            ga = psum.tile([P, BANK], F32, name="ga", tag="bank%d" % (4 * (t % 2) + 2 + h))
+            cols = slice(t % 2 * P, (t % 2 + 1) * P)
+            ga = psum.tile([P, BANK], F32, name="ga", tag="bank%d" % gate_bank[2 * t + h])
             for a in range(PASSES):
                 nc.tensor.matmul_mx(
                     out=ga[:],
-                    lhsT=wg_dealt[:, a, cols].bitcast(FP8X4),
+                    lhsT=wg_dealt[t // 2][:, a, cols].bitcast(FP8X4),
                     lhsT_scale=w_plane(0, a, t),
                     start=(a == 0),
                     stop=(a == PASSES - 1),
@@ -185,39 +193,64 @@ def tile_list_hwayt_dl_siluP_kernel(
                 )
             nc.scalar.activation(lean[t][:, halves[h]], ga[:], ACT.Tanh, bias=half_bias[:, t : t + 1], scale=0.5)
 
-        def feature_sum(t, h):
+        feature = {}
+
+        def feature_passes(t, h, first, last):
             cols = slice(t * P, (t + 1) * P)
-            ha = psum.tile([P, BANK], F32, name="ha", tag="bank%d" % (4 * (t % 2) + h))
+            if first == 0:
+                feature[t, h] = psum.tile([P, BANK], F32, name="ha", tag="bank%d" % feature_bank[2 * t + h])
             passes = [(wh4_dealt[:, a, cols].bitcast(U8).bitcast(FP4X4), w_plane(1, a, t), a) for a in range(PASSES)]
             part = slice((t % 2) * P, (t % 2 + 1) * P)
             passes += [
-                (whd_codes[:, t // 2, a, part].bitcast(FP8X4), whd_scales[:, t // 2, a, part], a) for a in range(PASSES)
+                (whd_codes[t // 2][:, a, part].bitcast(FP8X4), whd_scales[:, t // 2, a, part], a) for a in range(PASSES)
             ]
-            if t > 0:
+            if 2 * t + h >= EARLY:
                 passes = passes[::-1]
-            for i, (words, scale_bytes, a) in enumerate(passes):
+            for i in range(first, last):
+                words, scale_bytes, a = passes[i]
                 nc.tensor.matmul_mx(
-                    out=ha[:],
+                    out=feature[t, h][:],
                     lhsT=words,
                     lhsT_scale=scale_bytes,
                     start=(i == 0),
                     stop=(i == len(passes) - 1),
                     **moving(a, h),
                 )
-            nc.scalar.activation(made[t][:, halves[h]], ha[:], ACT.Silu)
+            if last == len(passes):
+                nc.scalar.activation(made[t][:, halves[h]], feature[t, h][:], ACT.Silu)
 
-        for t in range(PACK):
-            if t == 0:
-                for one_sum in (feature_sum, gate_sum):
-                    for h in range(HALVES):
-                        one_sum(t, h)
-            else:
-                for h in range(HALVES):
-                    feature_sum(t, h)
-                    gate_sum(t, h)
-            shares = zip(carry[t], halves) if t < PACK - 1 else zip(last_carry, chunks)
-            for share, js in shares:
-                nc.scalar.activation(share[:], lean[t][:, js], ACT.Copy, bias=0.5, scale=-0.5)
+        def carry_share(share, t, js):
+            nc.scalar.activation(share[:], lean[t][:, js], ACT.Copy, bias=0.5, scale=-0.5)
+
+        units = [divmod(k, HALVES) for k in range(PACK * HALVES)]
+        spare = psum.tile([P, BANK], F32, name="spare", tag="bank7")
+        for i in range(4):
+            nc.tensor.matmul_mx(
+                out=spare[:],
+                lhsT=wh4_dealt[:, 0, 0:P].bitcast(U8).bitcast(FP4X4),
+                lhsT_scale=w_rows[:, 1, :].bitcast(U8)[:, 0:P],
+                rhs=wh4_dealt[:, 0, :].bitcast(U8).bitcast(FP4X4),
+                rhs_scale=w_rows[:, 1, :].bitcast(U8),
+                start=True,
+                stop=True,
+            )
+        for first, last in ((0, 2), (2, 3)):
+            for h in range(HALVES):
+                feature_passes(0, h, first, last)
+        for t, h in units[:EARLY]:
+            gate_sum(t, h)
+        feature_passes(1, 0, 0, 3)
+        for t, h in units[:EARLY]:
+            feature_passes(t, h, 3, 4)
+        nc.vector.tensor_scalar(carry[0][0][:], lean[0][:, halves[0]], -0.5, 0.5, ALU.mult, ALU.add)
+        carry_share(carry[0][1], 0, halves[1])
+        for t, h in units[EARLY:]:
+            feature_passes(t, h, 0, 4)
+            gate_sum(t, h)
+            if h == HALVES - 1:
+                shares = zip(carry[t], halves) if t < PACK - 1 else zip(last_carry, chunks)
+                for share, js in shares:
+                    carry_share(share, t, js)
 
         y = keep.tile([P, PACK, J], F32, name="y")
         y_rows = out_0.rearrange("(p t) j -> p t j", t=PACK)
@@ -227,24 +260,26 @@ def tile_list_hwayt_dl_siluP_kernel(
 
         gated = {}
 
-        def gate_made(t, h):
-            if t == 0:
-                gated[t, h] = keep.tile([P, BANK], F32, name="gated0_%d" % h)
+        def gate_made(k):
+            t, h = units[k]
+            if k < EARLY:
+                gated[t, h] = keep.tile([P, BANK], F32, name="gated%d_%d" % (t, h))
             else:
-                at = 13 * T + 4 * J * (t - 1) + 2 * J * h
+                at = 13 * T + 2 * J * (k - EARLY)
                 gated[t, h] = laid.tile([P, BANK], F32, name="gated%d_%d" % (t, h), offset=at, align_bytes=64)
             js = halves[h]
             nc.vector.scalar_tensor_tensor(gated[t, h][:], lean[t][:, js], 1.0, made[t][:, js], ALU.add, ALU.mult)
 
-        for h in range(HALVES):
-            gate_made(0, h)
+        for k in range(EARLY):
+            gate_made(k)
         for t in range(PACK - 1):
             carried = keep.tile([P, J], F32, name="carried%d" % t, tag="carried%d" % (t % 2))
             for h, js in enumerate(halves):
                 nc.vector.tensor_tensor(carried[:, js], r_tiles[t][:].indirect(entries(js)), carry[t][h][:], ALU.mult)
             for h, js in enumerate(halves):
                 nc.vector.scalar_tensor_tensor(y[:, t, js], gated[t, h][:], 0.5, carried[:, js], ALU.mult, ALU.add)
-                gate_made(t + 1, h)
+                if HALVES * t + h + EARLY < len(units):
+                    gate_made(HALVES * t + h + EARLY)
             nc.sync.dma_start(y_rows[:, t, :], y[:, t, :])
         t = PACK - 1
 

@@ -58,13 +58,13 @@ def tile_list_hwayt_dl_siluP_kernel(
 
         tab = keep.tile([P, T], I32, name="tab", align_bytes=64)
         nc.sync.dma_start(tab[:], tab_words[0].rearrange("p c i -> p (c i)").bitcast(I32))
-        wh4_raw = keep.tile([P, PASSES, N // 2], I32, name="wh4_raw")
+        wh4_raw = keep.tile([P, PASSES, N // 2], I32, name="wh4_raw", align_bytes=64)
         nc.sync.dma_start(wh4_raw[:], wh4_words.rearrange("a p c -> p a c").bitcast(I32))
         whd_rows = whd.rearrange("(a p i) n -> a p (i n)", a=PASSES, i=PACK)
-        whd_first = laid.tile([P, PACK * N], F32, name="whd_first", offset=9 * T, align_bytes=64)
-        nc.sync.dma_start(whd_first[:], whd_rows[0])
+        wg_raw = keep.tile([P, PASSES, N], I32, name="wg_raw", align_bytes=64)
+        nc.sync.dma_start(wg_raw[:], wg_words.rearrange("a p n i -> p a (n i)").bitcast(I32))
 
-        spanning = laid.tile([P, T + J], U8, name="spanning", offset=4 * T - J // 2, align_bytes=64)
+        spanning = laid.tile([P, 2 * T + J], U8, name="spanning", offset=4 * T - J // 2, align_bytes=64)
         picked = spanning[:, 0:J]
         nc.vector.tensor_copy(picked, tab_rows[:].bitcast(U8).indirect(offsets[:]))
         staged = keep.tile([P, PLANE // 4], I32, name="staged", align_bytes=64)
@@ -73,39 +73,44 @@ def tile_list_hwayt_dl_siluP_kernel(
             w_rows[:].bitcast(U8).rearrange("p w (c i t) -> p w c t i", t=PACK, i=16),
         )
         nc.vector.tensor_copy(staged[:, 2 * N // 4 :], picked.bitcast(I32))
-        for q in range(4):
-            (nc.sync, nc.scalar)[q // 2].dma_start(planes[32 * q : 32 * q + 4, :], staged[ROWS_AT + 8 * q : ROWS_AT + 8 * q + 8, :])
+        for q in (0, 2, 1, 3):
+            nc.sync.dma_start(planes[32 * q : 32 * q + 4, :], staged[ROWS_AT + 8 * q : ROWS_AT + 8 * q + 8, :])
         plane_bytes = planes[:].bitcast(U8)
-        wg_raw = laid.tile([P, PASSES, N], I32, name="wg_raw", offset=4 * T, align_bytes=64)
-        nc.sync.dma_start(wg_raw[:], wg_words.rearrange("a p n i -> p a (n i)").bitcast(I32))
+        whd_first = laid.tile([P, PACK * N], F32, name="whd_first", offset=4 * T, align_bytes=64)
+        nc.sync.dma_start(whd_first[:], whd_rows[0])
         whd_second = laid.tile([P, PACK * N], F32, name="whd_second", offset=4 * T - 4 * PACK * N, align_bytes=64)
         nc.sync.dma_start(whd_second[:], whd_rows[1])
         whd_raw = (whd_first, whd_second)
         half_bias = keep.tile([P, PACK], F32, name="half_bias")
         nc.vector.tensor_scalar(half_bias[:], bias[:], 0.5, None, ALU.mult)
 
-        pairs, v_words = [], []
-        for h in range(HALVES):
-            pairs.append(keep.tile([P, BANK], I32, name="pairs%d" % h, tag="r%d" % (1 + h), align_bytes=64))
-            nc.vector.tensor_copy(
-                pairs[h][:].bitcast(U32), tab[:].bitcast(U32).indirect(offsets[:, h * 32 : (h + 1) * 32])
-            )
         wh4_dealt = keep.tile([P, PASSES, N], U16, name="wh4_dealt", align_bytes=64)
         for a in range(PASSES):
             nc.scalar.copy(
-                wh4_dealt[:, a, :].rearrange("p (t m) -> p m t", t=PACK),
-                wh4_raw[:, a, :].bitcast(U16).rearrange("p (m t) -> p m t", t=PACK),
+                wh4_dealt[:, a, :].rearrange("p (t c i) -> p c t i", t=PACK, i=8),
+                wh4_raw[:, a, :].bitcast(U16).rearrange("p (c i t) -> p c t i", t=PACK, i=8),
             )
+        wg_dealt = [keep.tile([P, PASSES, N // 2], U32, name="wg_dealt%d" % u, align_bytes=64) for u in range(2)]
+        for u in range(2):
+            nc.scalar.copy(
+                wg_dealt[u][:].rearrange("p a (t c i) -> p a c t i", t=2, i=4),
+                wg_raw[:].bitcast(U32).rearrange("p a (c i t) -> p a c t i", t=PACK, i=4)[:, :, :, 2 * u : 2 * u + 2, :],
+            )
+        v_words = []
         for h in range(HALVES):
+            pairs = keep.tile([P, BANK], I32, name="pairs%d" % h, tag="r1", align_bytes=64)
+            nc.vector.tensor_copy(
+                pairs[:].bitcast(U32), tab[:].bitcast(U32).indirect(offsets[:, h * 32 : (h + 1) * 32])
+            )
             parted = keep.tile([P, PASSES, BANK], U16, name="parted%d" % h, align_bytes=64)
-            nc.vector.tensor_copy(parted[:], pairs[h][:].bitcast(U16).rearrange("p (j d) -> p d j", d=PASSES))
+            nc.vector.tensor_copy(parted[:], pairs[:].bitcast(U16).rearrange("p (j d) -> p d j", d=PASSES))
             v_words.append(parted)
 
-        whd_codes = [keep.tile([P, PASSES, N // 2], U32, name="whd_codes0", align_bytes=64)]
+        whd_codes = keep.tile([P, 2, PASSES, N // 2], U32, name="whd_codes", align_bytes=64)
         whd_scales = keep.tile([P, 2, PASSES, N // 2], U8, name="whd_scales", align_bytes=64)
         whd_grouped = {
-            (a, u): keep.tile([P, 2 * N], BF16, name="whd_grouped%d_%d" % (a, u), align_bytes=64)
-            for a, u in ((0, 0), (0, 1))
+            (0, 0): keep.tile([P, 2 * N], BF16, name="whd_grouped0_0", tag="r2", align_bytes=64),
+            (0, 1): keep.tile([P, 2 * N], BF16, name="whd_grouped0_1", align_bytes=64),
         }
 
         def round_whd(copy, a, u):
@@ -115,24 +120,20 @@ def tile_list_hwayt_dl_siluP_kernel(
             )
 
         def quantise_whd(a, u):
-            nc.vector.quantize_mx(
-                out=whd_codes[u][:, a, :].bitcast(FP8X4), scales=whd_scales[:, u, a, :], in_=whd_grouped[a, u][:]
-            )
+            width = P if (a, u) == (1, 0) else 2 * P
+            for c0 in range(0, 2 * P, width):
+                nc.vector.quantize_mx(
+                    out=whd_codes[:, u, a, c0 : c0 + width].bitcast(FP8X4),
+                    scales=whd_scales[:, u, a, c0 : c0 + width],
+                    in_=whd_grouped[a, u][:, PACK * c0 : PACK * (c0 + width)],
+                )
 
-        round_whd(nc.scalar.copy, 0, 0)
-        quantise_whd(0, 0)
-        round_whd(nc.scalar.copy, 0, 1)
-        wg_dealt = [keep.tile([P, PASSES, N // 2], I32, name="wg_dealt%d" % u, align_bytes=64) for u in range(2)]
         for u in range(2):
-            nc.vector.tensor_copy(
-                wg_dealt[u][:].rearrange("p a (t m) -> p a m t", t=2),
-                wg_raw[:].rearrange("p a (m t) -> p a m t", t=PACK)[:, :, :, 2 * u : 2 * u + 2],
-            )
-        whd_codes.append(laid.tile([P, PASSES, N // 2], U32, name="whd_codes1", offset=4 * T, align_bytes=64))
-        quantise_whd(0, 1)
+            round_whd(nc.vector.tensor_copy, 0, u)
+            quantise_whd(0, u)
         for u in range(2):
             whd_grouped[1, u] = laid.tile(
-                [P, 2 * N], BF16, name="whd_grouped1_%d" % u, offset=13 * T + J + 3 * BANK * u, align_bytes=64
+                [P, 2 * N], BF16, name="whd_grouped1_%d" % u, offset=18 * T, align_bytes=64
             )
             round_whd(nc.vector.tensor_copy, 1, u)
             quantise_whd(1, u)
@@ -141,7 +142,7 @@ def tile_list_hwayt_dl_siluP_kernel(
         r_tiles = []
         for t in range(PACK):
             if t in (0, PACK - 1):
-                r_tile = laid.tile([P, T], F32, name="r_tile%d" % t, offset=5 * T if t == 0 else 0, align_bytes=64)
+                r_tile = laid.tile([P, T], F32, name="r_tile%d" % t, offset=6 * T if t == 0 else 0, align_bytes=64)
             else:
                 r_tile = keep.tile([P, T], F32, name="r_tile%d" % t, tag="r%d" % t, align_bytes=64)
             nc.sync.dma_start(r_tile[:], r_rows[:, t, :])
@@ -155,10 +156,10 @@ def tile_list_hwayt_dl_siluP_kernel(
             at = a * PLANE + w * N + t * P
             return plane_bytes[:, at : at + P]
 
-        lean = [laid.tile([P, J], F32, name="lean%d" % t, offset=9 * T + 4 * J * t, align_bytes=64) for t in range(PACK)]
+        lean = [laid.tile([P, J], F32, name="lean%d" % t, offset=10 * T + 4 * J * t, align_bytes=64) for t in range(PACK)]
         carry = [
             [
-                laid.tile([P, BANK], F32, name="carry%d_%d" % (t, h), offset=13 * T + 4 * J * t + 2 * J * h, align_bytes=64)
+                laid.tile([P, BANK], F32, name="carry%d_%d" % (t, h), offset=14 * T + 4 * J * t + 2 * J * h, align_bytes=64)
                 for h in range(HALVES)
             ]
             for t in range(PACK - 1)
@@ -168,16 +169,22 @@ def tile_list_hwayt_dl_siluP_kernel(
             j0 = chunks[-1].stop if chunks else 0
             chunks.append(slice(j0, j0 + width))
         last_carry = [
-            laid.tile([P, js.stop - js.start], F32, name="last_carry%d" % c, offset=16 * T + BANK * c, align_bytes=64)
+            laid.tile([P, js.stop - js.start], F32, name="last_carry%d" % c, offset=17 * T + BANK * c, align_bytes=64)
             for c, js in enumerate(chunks)
         ]
-        made = [keep.tile([P, J], F32, name="made%d" % t) for t in range(PACK)]
+        made = [
+            laid.tile([P, J], F32, name="made0", offset=15 * T, align_bytes=64)
+            if t == 0
+            else keep.tile([P, J], F32, name="made%d" % t)
+            for t in range(PACK)
+        ]
 
         halves = [slice(h * BANK, (h + 1) * BANK) for h in range(HALVES)]
 
-        feature_bank = (0, 1, 4, 5, 2, 3, 6, 7)
-        gate_bank = (2, 3, 6, 0, 1, 4, 5, 2)
+        feature_bank = (0, 1, 2, 3, 4, 5, 6, 7)
+        gate_bank = (4, 6, 5, 0, 1, 2, 3, 4)
         EARLY = 3
+        AHEAD = 3
 
         def gate_sum(t, h):
             cols = slice(t % 2 * P, (t % 2 + 1) * P)
@@ -202,10 +209,12 @@ def tile_list_hwayt_dl_siluP_kernel(
             passes = [(wh4_dealt[:, a, cols].bitcast(U8).bitcast(FP4X4), w_plane(1, a, t), a) for a in range(PASSES)]
             part = slice((t % 2) * P, (t % 2 + 1) * P)
             passes += [
-                (whd_codes[t // 2][:, a, part].bitcast(FP8X4), whd_scales[:, t // 2, a, part], a) for a in range(PASSES)
+                (whd_codes[:, t // 2, a, part].bitcast(FP8X4), whd_scales[:, t // 2, a, part], a) for a in range(PASSES)
             ]
             if 2 * t + h >= EARLY:
                 passes = passes[::-1]
+            elif t + h > 0:
+                passes = passes[:2] + passes[:1:-1]
             for i in range(first, last):
                 words, scale_bytes, a = passes[i]
                 nc.tensor.matmul_mx(
@@ -217,7 +226,10 @@ def tile_list_hwayt_dl_siluP_kernel(
                     **moving(a, h),
                 )
             if last == len(passes):
-                nc.scalar.activation(made[t][:, halves[h]], feature[t, h][:], ACT.Silu)
+                width = BANK // 2 if 2 * t + h == AHEAD - 1 else BANK
+                for j0 in range(0, BANK, width):
+                    js = slice(h * BANK + j0, h * BANK + j0 + width)
+                    nc.scalar.activation(made[t][:, js], feature[t, h][:, j0 : j0 + width], ACT.Silu)
 
         def carry_share(share, t, js):
             nc.scalar.activation(share[:], lean[t][:, js], ACT.Copy, bias=0.5, scale=-0.5)
@@ -234,16 +246,33 @@ def tile_list_hwayt_dl_siluP_kernel(
                 start=True,
                 stop=True,
             )
-        for first, last in ((0, 2), (2, 3)):
-            for h in range(HALVES):
-                feature_passes(0, h, first, last)
-        for t, h in units[:EARLY]:
+        for t, h in ((0, 0), (1, 0)):
+            feature_passes(t, h, 0, 2)
             gate_sum(t, h)
-        feature_passes(1, 0, 0, 3)
+        gate_sum(0, 1)
+        feature_passes(0, 1, 0, 2)
+        for h in range(HALVES):
+            carry_share(carry[0][h], 0, halves[h])
         for t, h in units[:EARLY]:
-            feature_passes(t, h, 3, 4)
-        nc.vector.tensor_scalar(carry[0][0][:], lean[0][:, halves[0]], -0.5, 0.5, ALU.mult, ALU.add)
-        carry_share(carry[0][1], 0, halves[1])
+            feature_passes(t, h, 2, 4)
+        gated = {}
+
+        def gate_made(k):
+            t, h = units[k]
+            if k < AHEAD:
+                gated[t, h] = keep.tile([P, BANK], F32, name="gated%d_%d" % (t, h))
+            else:
+                at = 14 * T + 2 * J * (k - AHEAD)
+                gated[t, h] = laid.tile([P, BANK], F32, name="gated%d_%d" % (t, h), offset=at, align_bytes=64)
+            width = BANK // 2 if k == AHEAD - 1 else BANK
+            for j0 in range(0, BANK, width):
+                js = slice(h * BANK + j0, h * BANK + j0 + width)
+                nc.vector.scalar_tensor_tensor(
+                    gated[t, h][:, j0 : j0 + width], lean[t][:, js], 1.0, made[t][:, js], ALU.add, ALU.mult
+                )
+
+        for k in range(AHEAD):
+            gate_made(k)
         for t, h in units[EARLY:]:
             feature_passes(t, h, 0, 4)
             gate_sum(t, h)
@@ -258,28 +287,14 @@ def tile_list_hwayt_dl_siluP_kernel(
         def entries(js):
             return offsets[:, js.start // 16 : js.stop // 16]
 
-        gated = {}
-
-        def gate_made(k):
-            t, h = units[k]
-            if k < EARLY:
-                gated[t, h] = keep.tile([P, BANK], F32, name="gated%d_%d" % (t, h))
-            else:
-                at = 13 * T + 2 * J * (k - EARLY)
-                gated[t, h] = laid.tile([P, BANK], F32, name="gated%d_%d" % (t, h), offset=at, align_bytes=64)
-            js = halves[h]
-            nc.vector.scalar_tensor_tensor(gated[t, h][:], lean[t][:, js], 1.0, made[t][:, js], ALU.add, ALU.mult)
-
-        for k in range(EARLY):
-            gate_made(k)
         for t in range(PACK - 1):
             carried = keep.tile([P, J], F32, name="carried%d" % t, tag="carried%d" % (t % 2))
             for h, js in enumerate(halves):
                 nc.vector.tensor_tensor(carried[:, js], r_tiles[t][:].indirect(entries(js)), carry[t][h][:], ALU.mult)
             for h, js in enumerate(halves):
                 nc.vector.scalar_tensor_tensor(y[:, t, js], gated[t, h][:], 0.5, carried[:, js], ALU.mult, ALU.add)
-                if HALVES * t + h + EARLY < len(units):
-                    gate_made(HALVES * t + h + EARLY)
+                if HALVES * t + h + AHEAD < len(units):
+                    gate_made(HALVES * t + h + AHEAD)
             nc.sync.dma_start(y_rows[:, t, :], y[:, t, :])
         t = PACK - 1
 
@@ -300,7 +315,7 @@ def tile_list_hwayt_dl_siluP_kernel(
 
         def look_up(c, js):
             kept[c] = laid.tile(
-                [P, js.stop - js.start], F32, name="kept%d" % c, offset=(9 * T + J * c if c < 2 else 16 * T + BANK * (c - 2)), align_bytes=64
+                [P, js.stop - js.start], F32, name="kept%d" % c, offset=(10 * T + J * c if c < 2 else 17 * T + BANK * (c - 2)), align_bytes=64
             )
             nc.vector.tensor_tensor(kept[c][:], r_tiles[t][:].indirect(entries(js)), last_carry[c][:], ALU.mult)
 

@@ -235,17 +235,6 @@ def tile_list_hwayt_dl_siluP_kernel(
             nc.scalar.activation(share[:], lean[t][:, js], ACT.Copy, bias=0.5, scale=-0.5)
 
         units = [divmod(k, HALVES) for k in range(PACK * HALVES)]
-        spare = psum.tile([P, BANK], F32, name="spare", tag="bank7")
-        for i in range(4):
-            nc.tensor.matmul_mx(
-                out=spare[:],
-                lhsT=wh4_dealt[:, 0, 0:P].bitcast(U8).bitcast(FP4X4),
-                lhsT_scale=w_rows[:, 1, :].bitcast(U8)[:, 0:P],
-                rhs=wh4_dealt[:, 0, :].bitcast(U8).bitcast(FP4X4),
-                rhs_scale=w_rows[:, 1, :].bitcast(U8),
-                start=True,
-                stop=True,
-            )
         for t, h in ((0, 0), (1, 0)):
             feature_passes(t, h, 0, 2)
             gate_sum(t, h)

from contextlib import ExitStack

import concourse.mybir as mybir

K, N, T, J = 1024, 512, 4096, 1024
FLOPS = 3 * 2 * K * N * J

F32 = mybir.dt.float32
BF16 = mybir.dt.bfloat16
I32 = mybir.dt.int32
U32 = mybir.dt.uint32
U16 = mybir.dt.uint16
U8 = mybir.dt.uint8
FP8X4 = mybir.dt.float8_e4m3fn_x4
FP4X4 = mybir.dt.float4_e2m1fn_x4
ALU = mybir.AluOpType
ACT = mybir.ActivationFunctionType

P = 128
PACK = 4
PASSES = K // (P * PACK)
BANK = 512
HALVES = J // BANK
ROWS_AT = 96
PLANE = 2 * N + J
LAST_CHUNKS = (128,) * 8
CODE_CHUNKS = (256, 256, 256, 128, 128)
STORE_FROM = {512: 0, 768: 512, 1024: 768}


def tile_list_hwayt_dl_siluP_kernel(
    tc, tab_words, tab_scales, wg_words, wg_scales, wh4_words, wh4_scales, whd, bg, rT, offs, out_0, out_1, out_2
):
    nc = tc.nc
    with ExitStack() as ctx:
        keep = ctx.enter_context(tc.tile_pool(name="keep", bufs=1))
        laid = ctx.enter_context(tc.tile_pool(name="laid", bufs=1))
        psum = ctx.enter_context(tc.psum_pool(name="psum", bufs=1))

        offsets = keep.tile([P, J // 16], U16, name="offsets")
        tab_rows = keep.tile([P, T // 4], I32, name="tab_rows", align_bytes=64)
        nc.vector.memset(tab_rows[0:ROWS_AT, :], 0)
        nc.sync.dma_start(tab_rows[ROWS_AT:P, :], tab_scales.bitcast(I32).rearrange("a q c -> q a c"))
        nc.sync.dma_start(offsets[:], offs)
        w_rows = keep.tile([P, 2, N // 4], I32, name="w_rows", align_bytes=64)
        nc.vector.memset(w_rows[0:ROWS_AT, :, :], 0)
        for w, scales in enumerate((wg_scales, wh4_scales)):
            nc.sync.dma_start(w_rows[ROWS_AT:P, w, :], scales.bitcast(I32).rearrange("a q c -> q a c"))
        planes = keep.tile([P, PASSES * PLANE // 4], I32, name="planes", align_bytes=64)
        nc.vector.memset(planes[:], 0)

        bias = keep.tile([P, PACK], F32, name="bias")
        nc.scalar.dma_start(bias[:], bg.rearrange("(p t) -> p t", t=PACK))
        warm = keep.tile([P, 1], F32, name="warm")
        warm_out = keep.tile([P, 1], F32, name="warm_out")
        nc.vector.memset(warm[:], 0.0)
        nc.scalar.activation(warm_out[:], warm[:], ACT.Silu)

        tab = keep.tile([P, T], I32, name="tab", align_bytes=64)
        nc.sync.dma_start(tab[:], tab_words[0].rearrange("p c i -> p (c i)").bitcast(I32))
        wh4_raw = keep.tile([P, PASSES, N // 2], I32, name="wh4_raw", align_bytes=64)
        nc.sync.dma_start(wh4_raw[:], wh4_words.rearrange("a p c -> p a c").bitcast(I32))
        whd_rows = whd.rearrange("(a p i) n -> a p (i n)", a=PASSES, i=PACK)
        wg_raw = keep.tile([P, PASSES, N], I32, name="wg_raw", align_bytes=64)
        nc.sync.dma_start(wg_raw[:], wg_words.rearrange("a p n i -> p a (n i)").bitcast(I32))

        spanning = laid.tile([P, 2 * T + J], U8, name="spanning", offset=4 * T - J // 2, align_bytes=64)
        picked = spanning[:, 0:J]
        nc.vector.tensor_copy(picked, tab_rows[:].bitcast(U8).indirect(offsets[:]))
        staged = keep.tile([P, PLANE // 4], I32, name="staged", align_bytes=64)
        nc.vector.tensor_copy(
            staged[:, 0 : 2 * N // 4].bitcast(U8).rearrange("p (w t c i) -> p w c t i", w=2, t=PACK, i=16),
            w_rows[:].bitcast(U8).rearrange("p w (c i t) -> p w c t i", t=PACK, i=16),
        )
        nc.vector.tensor_copy(staged[:, 2 * N // 4 :], picked.bitcast(I32))
        for q in (0, 2, 1, 3):
            nc.sync.dma_start(planes[32 * q : 32 * q + 4, :], staged[ROWS_AT + 8 * q : ROWS_AT + 8 * q + 8, :])
        plane_bytes = planes[:].bitcast(U8)
        whd_first = laid.tile([P, PACK * N], F32, name="whd_first", offset=4 * T, align_bytes=64)
        nc.sync.dma_start(whd_first[:], whd_rows[0])
        whd_second = laid.tile([P, PACK * N], F32, name="whd_second", offset=4 * T - 4 * PACK * N, align_bytes=64)
        nc.sync.dma_start(whd_second[:], whd_rows[1])
        whd_raw = (whd_first, whd_second)
        half_bias = keep.tile([P, PACK], F32, name="half_bias")
        nc.vector.tensor_scalar(half_bias[:], bias[:], 0.5, None, ALU.mult)

        wh4_dealt = keep.tile([P, PASSES, N], U16, name="wh4_dealt", align_bytes=64)
        for a in range(PASSES):
            nc.scalar.copy(
                wh4_dealt[:, a, :].rearrange("p (t c i) -> p c t i", t=PACK, i=8),
                wh4_raw[:, a, :].bitcast(U16).rearrange("p (c i t) -> p c t i", t=PACK, i=8),
            )
        wg_dealt = [keep.tile([P, PASSES, N // 2], U32, name="wg_dealt%d" % u, align_bytes=64) for u in range(2)]
        for u in range(2):
            nc.scalar.copy(
                wg_dealt[u][:].rearrange("p a (t c i) -> p a c t i", t=2, i=4),
                wg_raw[:].bitcast(U32).rearrange("p a (c i t) -> p a c t i", t=PACK, i=4)[:, :, :, 2 * u : 2 * u + 2, :],
            )
        v_words = []
        for h in range(HALVES):
            pairs = keep.tile([P, BANK], I32, name="pairs%d" % h, tag="r1", align_bytes=64)
            nc.vector.tensor_copy(
                pairs[:].bitcast(U32), tab[:].bitcast(U32).indirect(offsets[:, h * 32 : (h + 1) * 32])
            )
            parted = keep.tile([P, PASSES, BANK], U16, name="parted%d" % h, align_bytes=64)
            nc.vector.tensor_copy(parted[:], pairs[:].bitcast(U16).rearrange("p (j d) -> p d j", d=PASSES))
            v_words.append(parted)

        whd_codes = keep.tile([P, 2, PASSES, N // 2], U32, name="whd_codes", align_bytes=64)
        whd_scales = keep.tile([P, 2, PASSES, N // 2], U8, name="whd_scales", align_bytes=64)
        whd_grouped = {
            (0, 0): keep.tile([P, 2 * N], BF16, name="whd_grouped0_0", tag="r2", align_bytes=64),
            (0, 1): keep.tile([P, 2 * N], BF16, name="whd_grouped0_1", align_bytes=64),
        }

        def round_whd(copy, a, u):
            copy(
                whd_grouped[a, u][:].rearrange("p (t m i) -> p m i t", t=2, i=PACK),
                whd_raw[a][:].rearrange("p (i m t) -> p m i t", i=PACK, t=PACK)[:, :, :, 2 * u : 2 * u + 2],
            )

        def quantise_whd(a, u):
            width = P if (a, u) == (1, 0) else 2 * P
            for c0 in range(0, 2 * P, width):
                nc.vector.quantize_mx(
                    out=whd_codes[:, u, a, c0 : c0 + width].bitcast(FP8X4),
                    scales=whd_scales[:, u, a, c0 : c0 + width],
                    in_=whd_grouped[a, u][:, PACK * c0 : PACK * (c0 + width)],
                )

        for u in range(2):
            round_whd(nc.vector.tensor_copy, 0, u)
            quantise_whd(0, u)
        for u in range(2):
            whd_grouped[1, u] = laid.tile(
                [P, 2 * N], BF16, name="whd_grouped1_%d" % u, offset=18 * T, align_bytes=64
            )
            round_whd(nc.vector.tensor_copy, 1, u)
            quantise_whd(1, u)

        r_rows = rT.rearrange("(p t) c -> p t c", t=PACK)
        r_tiles = []
        for t in range(PACK):
            if t in (0, PACK - 1):
                r_tile = laid.tile([P, T], F32, name="r_tile%d" % t, offset=6 * T if t == 0 else 0, align_bytes=64)
            else:
                r_tile = keep.tile([P, T], F32, name="r_tile%d" % t, tag="r%d" % t, align_bytes=64)
            nc.sync.dma_start(r_tile[:], r_rows[:, t, :])
            r_tiles.append(r_tile)

        def moving(a, h):
            at = a * PLANE + 2 * N + h * BANK
            return dict(rhs=v_words[h][:, a, :].bitcast(U8).bitcast(FP4X4), rhs_scale=plane_bytes[:, at : at + BANK])

        def w_plane(w, a, t):
            at = a * PLANE + w * N + t * P
            return plane_bytes[:, at : at + P]

        lean = [laid.tile([P, J], F32, name="lean%d" % t, offset=10 * T + 4 * J * t, align_bytes=64) for t in range(PACK)]
        carry = [
            [
                laid.tile([P, BANK], F32, name="carry%d_%d" % (t, h), offset=14 * T + 4 * J * t + 2 * J * h, align_bytes=64)
                for h in range(HALVES)
            ]
            for t in range(PACK - 1)
        ]
        chunks = []
        for width in LAST_CHUNKS:
            j0 = chunks[-1].stop if chunks else 0
            chunks.append(slice(j0, j0 + width))
        last_carry = [
            laid.tile([P, js.stop - js.start], F32, name="last_carry%d" % c, offset=17 * T + BANK * c, align_bytes=64)
            for c, js in enumerate(chunks)
        ]
        made = [
            laid.tile([P, J], F32, name="made0", offset=15 * T, align_bytes=64)
            if t == 0
            else keep.tile([P, J], F32, name="made%d" % t)
            for t in range(PACK)
        ]

        halves = [slice(h * BANK, (h + 1) * BANK) for h in range(HALVES)]

        feature_bank = (0, 1, 2, 3, 4, 5, 6, 7)
        gate_bank = (4, 6, 5, 0, 1, 2, 3, 4)
        EARLY = 3
        AHEAD = 3

        def gate_sum(t, h):
            cols = slice(t % 2 * P, (t % 2 + 1) * P)
            ga = psum.tile([P, BANK], F32, name="ga", tag="bank%d" % gate_bank[2 * t + h])
            for a in range(PASSES):
                nc.tensor.matmul_mx(
                    out=ga[:],
                    lhsT=wg_dealt[t // 2][:, a, cols].bitcast(FP8X4),
                    lhsT_scale=w_plane(0, a, t),
                    start=(a == 0),
                    stop=(a == PASSES - 1),
                    **moving(a, h),
                )
            nc.scalar.activation(lean[t][:, halves[h]], ga[:], ACT.Tanh, bias=half_bias[:, t : t + 1], scale=0.5)

        feature = {}

        def feature_passes(t, h, first, last):
            cols = slice(t * P, (t + 1) * P)
            if first == 0:
                feature[t, h] = psum.tile([P, BANK], F32, name="ha", tag="bank%d" % feature_bank[2 * t + h])
            passes = [(wh4_dealt[:, a, cols].bitcast(U8).bitcast(FP4X4), w_plane(1, a, t), a) for a in range(PASSES)]
            part = slice((t % 2) * P, (t % 2 + 1) * P)
            passes += [
                (whd_codes[:, t // 2, a, part].bitcast(FP8X4), whd_scales[:, t // 2, a, part], a) for a in range(PASSES)
            ]
            if 2 * t + h >= EARLY:
                passes = passes[::-1]
            elif t + h > 0:
                passes = passes[:2] + passes[:1:-1]
            for i in range(first, last):
                words, scale_bytes, a = passes[i]
                nc.tensor.matmul_mx(
                    out=feature[t, h][:],
                    lhsT=words,
                    lhsT_scale=scale_bytes,
                    start=(i == 0),
                    stop=(i == len(passes) - 1),
                    **moving(a, h),
                )
            if last == len(passes):
                width = BANK // 2 if 2 * t + h == AHEAD - 1 else BANK
                for j0 in range(0, BANK, width):
                    js = slice(h * BANK + j0, h * BANK + j0 + width)
                    nc.scalar.activation(made[t][:, js], feature[t, h][:, j0 : j0 + width], ACT.Silu)

        def carry_share(share, t, js):
            nc.scalar.activation(share[:], lean[t][:, js], ACT.Copy, bias=0.5, scale=-0.5)

        units = [divmod(k, HALVES) for k in range(PACK * HALVES)]
        for t, h in ((0, 0), (1, 0)):
            feature_passes(t, h, 0, 2)
            gate_sum(t, h)
        gate_sum(0, 1)
        feature_passes(0, 1, 0, 2)
        for h in range(HALVES):
            carry_share(carry[0][h], 0, halves[h])
        for t, h in units[:EARLY]:
            feature_passes(t, h, 2, 4)
        gated = {}

        def gate_made(k):
            t, h = units[k]
            if k < AHEAD:
                gated[t, h] = keep.tile([P, BANK], F32, name="gated%d_%d" % (t, h))
            else:
                at = 14 * T + 2 * J * (k - AHEAD)
                gated[t, h] = laid.tile([P, BANK], F32, name="gated%d_%d" % (t, h), offset=at, align_bytes=64)
            width = BANK // 2 if k == AHEAD - 1 else BANK
            for j0 in range(0, BANK, width):
                js = slice(h * BANK + j0, h * BANK + j0 + width)
                nc.vector.scalar_tensor_tensor(
                    gated[t, h][:, j0 : j0 + width], lean[t][:, js], 1.0, made[t][:, js], ALU.add, ALU.mult
                )

        for k in range(AHEAD):
            gate_made(k)
        for t, h in units[EARLY:]:
            feature_passes(t, h, 0, 4)
            gate_sum(t, h)
            if h == HALVES - 1:
                shares = zip(carry[t], halves) if t < PACK - 1 else zip(last_carry, chunks)
                for share, js in shares:
                    carry_share(share, t, js)

        y = keep.tile([P, PACK, J], F32, name="y")
        y_rows = out_0.rearrange("(p t) j -> p t j", t=PACK)

        def entries(js):
            return offsets[:, js.start // 16 : js.stop // 16]

        for t in range(PACK - 1):
            carried = keep.tile([P, J], F32, name="carried%d" % t, tag="carried%d" % (t % 2))
            for h, js in enumerate(halves):
                nc.vector.tensor_tensor(carried[:, js], r_tiles[t][:].indirect(entries(js)), carry[t][h][:], ALU.mult)
            for h, js in enumerate(halves):
                nc.vector.scalar_tensor_tensor(y[:, t, js], gated[t, h][:], 0.5, carried[:, js], ALU.mult, ALU.add)
                if HALVES * t + h + AHEAD < len(units):
                    gate_made(HALVES * t + h + AHEAD)
            nc.sync.dma_start(y_rows[:, t, :], y[:, t, :])
        t = PACK - 1

        y_codes = keep.tile([P, J], I32, name="y_codes", align_bytes=64)
        y_scales = keep.tile([P, J], U8, name="y_scales", align_bytes=64)
        code_rows = out_1[0].rearrange("p j i -> p (j i)").bitcast(I32)
        kept = {}
        rounded = keep.tile([P, J * PACK], BF16, name="rounded", align_bytes=64)

        def round_pair(c, js, u):
            nc.scalar.copy(
                rounded[:].rearrange("p (j t) -> p j t", t=PACK)[:, js, 2 * u : 2 * u + 2],
                y[:, 2 * u : 2 * u + 2, js].rearrange("p t j -> p j t"),
            )

        for c, js in enumerate(halves):
            round_pair(c, js, 0)

        def look_up(c, js):
            kept[c] = laid.tile(
                [P, js.stop - js.start], F32, name="kept%d" % c, offset=(10 * T + J * c if c < 2 else 17 * T + BANK * (c - 2)), align_bytes=64
            )
            nc.vector.tensor_tensor(kept[c][:], r_tiles[t][:].indirect(entries(js)), last_carry[c][:], ALU.mult)

        def combine(c, js):
            at = js.start % BANK
            share = gated[t, js.start // BANK][:, at : at + js.stop - js.start]
            nc.vector.scalar_tensor_tensor(y[:, t, js], share, 0.5, kept[c][:], ALU.mult, ALU.add)
            round_pair(c, js, 1)
            if js.stop in STORE_FROM:
                ss = slice(STORE_FROM[js.stop], js.stop)
                nc.sync.dma_start(y_rows[:, t, ss], y[:, t, ss])

        def quantise(c, js):
            nc.vector.quantize_mx(out=y_codes[:, js].bitcast(FP8X4), scales=y_scales[:, js], in_=rounded[:, PACK * js.start : PACK * js.stop])
            if js.stop in STORE_FROM:
                ss = slice(STORE_FROM[js.stop], js.stop)
                nc.sync.dma_start(code_rows[:, ss], y_codes[:, ss])

        for c in range(len(chunks) + 1):
            if c < len(chunks):
                look_up(c, chunks[c])
            if c >= 1:
                combine(c - 1, chunks[c - 1])
        j0 = 0
        for c, width in enumerate(CODE_CHUNKS):
            quantise(c, slice(j0, j0 + width))
            j0 = j0 + width
        for q in range(4):
            queue = nc.scalar if q % 2 else nc.sync
            queue.dma_start(
                out_2[0, 4 * q : 4 * q + 4, :].bitcast(I32), y_scales[32 * q : 32 * q + 4, :].bitcast(I32)
            )
